import numpy as np, ml_dtypes
CORES = [16,18,20,22]
N = 4
BF = ml_dtypes.bfloat16
def gentries(a):
    return np.ascontiguousarray(a.reshape(8, 16, -1).transpose(0, 2, 1)).reshape(8, -1)
def gtable(e):
    e = np.asarray(e); return np.ascontiguousarray(e.reshape(8, -1, 16).transpose(0, 2, 1)).reshape(128, -1).astype(np.int32)
def f(rng, *shape):
    return (rng.standard_normal(shape, dtype=np.float32) * np.exp2(rng.integers(-2, 3, shape[:-1] + (1,)))).astype(BF)
def wide(rng, *shape):
    v = f(rng, *shape).astype(np.float32); k = shape[:-2] + (1, shape[-1])
    return (v * np.exp2(rng.integers(-6, 7, k)) * (rng.random(k) > 0.0625)).astype(BF)
M, S, D, Q = 4096, 64, 8, 2
P = N // Q
def forest(rng, L, aside, bushy, zero=False):
    free = S + rng.permutation(M - S); n = S * (D - 1)
    chain = np.concatenate([np.arange(S)[:, None], free[:n].reshape(S, D - 1)], 1)
    p = np.arange(M); dep = np.full(M, -1); dep[chain] = np.arange(D); p[chain[:, 1:]] = chain[:, :-1]; rest = free[n:]
    if bushy:
        h = len(rest) // 2; p[rest[:h]] = rng.integers(0, S); p[rest[h:]] = chain[rng.integers(0, S), D - 2]
    else:
        lev = rng.integers(1, D, len(rest))
        for d in range(1, D):
            v = rest[lev == d]; p[v] = rng.choice(np.flatnonzero(dep == d - 1), len(v)); dep[v] = d
    kids = S + rng.permutation(M - S); o = kids[np.argsort(p[kids], kind="stable")]; q = p[o]
    sib = np.zeros(M, np.int64); sib[o] = np.arange(M - S) - np.searchsorted(q, q); c = np.bincount(q, minlength=M)
    base = rng.integers(0, 4096, M); step = 2 * rng.integers(0, 2048, M) + 1
    if zero: base[0] = 0
    x = np.where((c > 0) & (rng.random(M) < 0.7), (rng.random(M) * c).astype(np.int64), c + (rng.random(M) * (4096 - c)).astype(np.int64))
    x[chain[:, :-1]] = sib[chain[:, 1:]]
    e = np.flatnonzero(L < D - 1); b = chain[e, L[e]]; w = sib[chain[e, L[e] + 1]]; cb = c[b]
    other = (w + 1 + (rng.random(len(e)) * (cb - 1)).astype(np.int64)) % cb; none = cb + (rng.random(len(e)) * (4096 - cb)).astype(np.int64)
    x[b] = np.where((cb > 1) & (rng.random(len(e)) < aside), other, none)
    t = (base + step * x) % 4096
    k = np.zeros(M, np.int64); k[o] = (base[q] + step[q] * sib[o]) % 4096
    k[:S] = np.where(rng.random(S) < 0.5, t[:S], rng.integers(0, 4096, S))
    return p, k, t
def shards(rng, t, sc, tie):
    v = sc * 4096 + t; win = rng.integers(0, N, t.shape); u = rng.random((N,) + t.shape)
    o = np.where(rng.random(t.shape) < tie, sc * 4096 + (u * (t + 1)).astype(np.int64), (u * (v + 1)).astype(np.int64))
    o = np.where((np.arange(N)[:, None, None, None] == win) | (rng.random(o.shape) < 0.03125), v, np.minimum(o, v))
    return np.ascontiguousarray(o.transpose(0, 2, 1, 3)).reshape(N, 8, N * M).astype(np.int32)
def draw(rng, L, aside=0.5, bushy=False, tie=0.125, uneven=False, zero=False):
    a = [[forest(rng, L[q, g], aside, bushy, zero) for g in range(8)] for q in range(N)]
    p, k, t = [np.array([[a[q][g][i] for g in range(8)] for q in range(N)]) for i in range(3)]
    sc = rng.integers(0, 4096, t.shape)
    if uneven: sc = 4095 >> rng.integers(0, 13, t.shape)
    return {"par": np.stack([gtable(p[q]) for q in range(N)]), "tok": k.astype(np.int32), "best": shards(rng, t, sc, tie), "kv": f(rng, N, 128, Q * M)}
def setup_inputs(rng):
    return draw(rng, rng.integers(0, D, (N, 8, S)))
def setup_inputs_full(rng):
    return draw(rng, np.full((N, 8, S), D - 1))
def setup_inputs_cut(rng):
    return draw(rng, rng.choice(np.array([0, 1, D - 2]), (N, 8, S)), aside=0.0, zero=True)
def setup_inputs_ties(rng):
    return draw(rng, rng.integers(0, D, (N, 8, S)), tie=1.0)
def setup_inputs_bushy(rng):
    return draw(rng, rng.integers(0, D, (N, 8, S)), bushy=True)
def setup_inputs_spread(rng):
    d = draw(rng, rng.integers(0, D, (N, 8, S)), uneven=True); d["kv"] = wide(rng, N, 128, Q * M); return d
def check_inputs(d):
    bad = []; p = np.stack([gentries(a) for a in d["par"]]).astype(np.int64); k = d["tok"].astype(np.int64); b = d["best"]
    if not np.isfinite(d["kv"].astype(np.float32)).all(): bad.append("finite")
    if b.min() < 0 or b.max() >= 1 << 24: bad.append("best")
    if k.min() < 0 or k.max() > 4095: bad.append("tokens")
    if p.min() < 0 or p.max() >= M: return bad + ["parents"]
    if (p[:, :, :S] != np.arange(S)).any(): bad.append("roots")
    a = p
    for i in range(D - 2): a = np.take_along_axis(p, a, 2)
    if (a >= S).any(): bad.append("depth")
    w = np.sort((p * 4096 + k)[:, :, S:], axis=2)
    if (w[:, :, 1:] == w[:, :, :-1]).any(): bad.append("children")
    return bad
def reference(par, tok, best, kv):
    p = np.stack([gentries(a) for a in par]).astype(np.int64)
    t = np.max(best, axis=0).reshape(8, N, M).transpose(1, 0, 2) & 4095
    ok = (np.arange(M) < S) | (tok == np.take_along_axis(t, p, 2))
    a = np.broadcast_to(np.arange(M), p.shape); acc = np.ones(p.shape, bool); dep = np.zeros(p.shape, np.int64)
    for i in range(D):
        acc = acc & np.take_along_axis(ok, a, 2); dep = dep + (a >= S); a = np.take_along_axis(p, a, 2)
    y = np.zeros((N, 128, Q * S * D), BF)
    for r in range(N):
        out = y[r].reshape(8, 16, Q * S * D)
        for i in range(Q):
            q = P * i + r % P; k = kv[r][:, i * M:(i + 1) * M].reshape(8, 16, M)
            g, j = np.nonzero(acc[q])
            out[g, :, (i * S + a[q, g, j]) * D + dep[q, g, j]] = k[g, :, j]
    return {"y": y}

@@ -1,0 +1,296 @@
+from concourse.bass import DstId, RemoteDMATransfer
+from concourse.mybir import AluOpType as A, AxisListType, ActivationFunctionType as F
+
+NSC = 176
+CHUNKS = [(4, 36), (36, 88), (88, 176), (176, 216), (216, 256)]
+W = 4112
+WD = 8320
+SCRATCH = {
+    "bs": ("sbuf", [128, 1024], "int32"),
+    "land": ("sbuf", [128, 1024], "int32"),
+    "pr": ("sbuf", [128, 256], "int32"),
+    "tk": ("sbuf", [128, 256], "int32"),
+    "hi32": ("sbuf", [128, 256], "int32"),
+    "lo32": ("sbuf", [128, 256], "int32"),
+    "hif": ("sbuf", [128, 256], "float16"),
+    "parc": ("sbuf", [128, 256], "float16"),
+    "offl": ("sbuf", [128, 256], "uint16"),
+    "tok2": ("sbuf", [128, 512], "float16"),
+    "hx": ("sbuf", [128, 4096], "float16"),
+    "key": ("sbuf", [128, 4096], "float32"),
+    "xx": ("sbuf", [128, 4096], "bfloat16"),
+    "mxi": ("sbuf", [128, 256], "int32"),
+    "tgt": ("sbuf", [128, 256], "int32"),
+    "pI": ("sbuf", [128, 1], "int32"),
+    "ki": ("sbuf", [128, 8], "int32"),
+    "kf": ("sbuf", [128, 8], "float32"),
+    "ev": ("sbuf", [128, 1], "float32"),
+    "bias": ("sbuf", [128, 1], "float32"),
+    "r16": ("sbuf", [128, 16], "bfloat16"),
+    "eq16": ("sbuf", [128, 16], "float32"),
+    "e2": ("sbuf", [128, 8], "float32"),
+    "mg": ("sbuf", [128, 128], "bfloat16"),
+    "mm": ("sbuf", [128, 128], "bfloat16"),
+    "t1": ("sbuf", [128, 128], "bfloat16"),
+    "ident": ("sbuf", [128, 128], "float16"),
+    "b4": ("sbuf", [128, 128], "float16"),
+    "sel2": ("sbuf", [128, 1024], "float16"),
+    "blk": ("sbuf", [128, 2048], "bfloat16"),
+    "s64": ("sbuf", [128, 64], "bfloat16"),
+    "mask": ("sbuf", [128, 64], "float32"),
+    "r4": ("sbuf", [128, 4], "float32"),
+    "dumpm": ("sbuf", [128, 256], "float32"),
+    "vals": ("sbuf", [128, NSC * 16], "float32"),
+    "zt": ("sbuf", [128, 514], "float32"),
+    "uu": ("sbuf", [128, 256], "float32"),
+    "off": ("sbuf", [128, 256], "uint16"),
+    "ns": ("sbuf", [128, WD], "float32"),
+    "nv": ("sbuf", [128, WD], "float32"),
+    "rm": ("sbuf", [128, 128], "float32"),
+    "rd": ("sbuf", [128, 4], "float32"),
+    "ofw": ("sbuf", [128, 32], "uint16"),
+    "la": ("sbuf", [128, 20], "uint16"),
+    "lb": ("sbuf", [128, 8], "uint16"),
+    "kvo": ("sbuf", [128, W], "bfloat16"),
+    "kvp": ("sbuf", [128, W], "bfloat16"),
+    "yy": ("sbuf", [128, 1024], "bfloat16"),
+    "pmx": ("psum", [128, 512], "float32"),
+}
+for _i in range(4):
+    SCRATCH["pk%d" % _i] = ("psum", [128, 512], "float32")
+for _i in range(3):
+    SCRATCH["pz%d" % _i] = ("psum", [128, 512], "float32")
+SEMAPHORES = (["vq", "sq", "tq", "gq", "sent", "lsent", "arA", "arB", "ldpar", "ldtok", "kva", "kvb", "zf", "st"]
+              + ["ld%d" % i for i in range(4)] + ["arr%d" % i for i in range(4)])
+
+
+def bits(engines):
+    m = 0
+    for e in engines:
+        m |= 1 << e
+    return m
+
+
+def rank_program(g, core, T, topo):
+    rank = T.rank_of(core)
+    if rank is None:
+        return
+    N = len(T.cores)
+    mate = (rank + 2) % N
+    io, ip = rank // 2, mate // 2
+    Q = {"v": g.vector, "s": g.scalar, "t": g.tensor, "g": g, "y": g.sync}
+    SN = {"v": "vq", "s": "sq", "t": "tq", "g": "gq"}
+    cnt = {"v": 0, "s": 0, "t": 0, "g": 0}
+    seen = {q: {} for q in Q}
+
+    def need(q, *deps):
+        for sem, val in deps:
+            if seen[q].get(sem, 0) < val:
+                Q[q].wait_ge(T.sem[sem], val)
+                seen[q][sem] = val
+
+    def do(q, deps, fn, *args, **kw):
+        need(q, *deps)
+        fn(*args, **kw).then_inc(T.sem[SN[q]], 1)
+        cnt[q] += 1
+        return (SN[q], cnt[q])
+
+    def V(deps, name, *args, **kw):
+        v = g.vector
+        fn = {"copy": v.tensor_copy, "tt": v.tensor_tensor, "ts": v.tensor_scalar, "red": v.tensor_reduce,
+              "set": v.memset}[name]
+        return do("v", deps, fn, *args, **kw)
+
+    def S(deps, *args, **kw):
+        return do("s", deps, g.scalar.activation, *args, **kw)
+
+    def P(deps, *args):
+        return do("t", deps, g.tensor.matmul, *args)
+
+    peers = [r for r in range(N) if r != rank]
+    far = [mate] + [r for r in peers if r != mate and topo.die(T.cores[r]) != topo.die(core)]
+    near = [r for r in peers if r not in far]
+    order = far + near
+    eng = {}
+    es = topo.engines(core, T.cores[mate])
+    step = len(es) // 2
+    eng[order[0]] = es[0:step:2]
+    eng[order[1]] = es[step:2 * step:2]
+    eng[order[2]] = es[1:step:2]
+    list_mask = bits(eng[order[0]] + eng[order[1]])
+    n_list = len(eng[order[0]] + eng[order[1]])
+
+    for r in order + [rank]:
+        g.sync.dma_start(T.bs[:, r * 256:(r + 1) * 256], T.best[:, r * 4096:(r + 1) * 4096]).then_inc(T.sem["ld%d" % r], 16)
+    g.scalar.dma_start(T.pr[:], T.par[:]).then_inc(T.sem.ldpar, 16)
+    g.scalar.dma_start(T.tk[:], T.tok[:]).then_inc(T.sem.ldtok, 16)
+
+    fl = {"allow_small_or_imprecise_dtypes": True}
+    i_p = do("g", [], g.iota, T.pI[:], [[1, 1]], 0, 1)
+    i_r16 = do("g", [], g.iota, T.r16[:], [[1, 16]], 0, 0, **fl)
+    i_mg = do("g", [], g.iota, T.mg[:], [[1, 8], [0, 16]], 0, 0, **fl)
+    i_mm = do("g", [], g.iota, T.mm[:], [[1, 128]], 0, 0, **fl)
+    i_v0 = do("g", [], g.iota, T.vals[:, 64:576], [[1, 512]], 65, 0, **fl)
+    need("g", *[("ld%d" % r, 16) for r in order])
+    tr = []
+    for r in order:
+        rid, pid, _ = topo.addr(T.cores[r])
+        tr.append(RemoteDMATransfer(dst_ids=[DstId(rid=rid, pnc=pid)], dma_engine_mask=bits(eng[r]),
+                                    remote_sem=T.sem["arr%d" % rank], src=T.bs[:, r * 256:(r + 1) * 256],
+                                    dst=T.land[:, rank * 256:(rank + 1) * 256]))
+    g.remote_dma_fused(tr, local_sem=T.sem.sent)
+    n_sent = sum(len(eng[r]) for r in order)
+    n_arr = len(eng[order[0]])
+    i_dm = do("g", [], g.iota, T.dumpm[:], [[16, 256]], -14336, 1, **fl)
+    i_s64 = do("g", [], g.iota, T.s64[:], [[0, 4], [1, 16]], 0, 0, **fl)
+    i_r4 = do("g", [], g.iota, T.r4[:], [[16, 4]], 16, 0, **fl)
+    i_v1 = do("g", [], g.iota, T.vals[:, 576:88 * 16], [[1, 88 * 16 - 576]], 577, 0, **fl)
+    i_v2 = do("g", [], g.iota, T.vals[:, 88 * 16:NSC * 16], [[1, (NSC - 88) * 16]], 88 * 16 + 1, 0, **fl)
+    i_nv = do("g", [], g.iota, T.nv[:, 2056:W], [[0, W - 2056]], 0, 0, **fl)
+
+    c_zt = V([], "set", T.zt[:], 0.0)
+    V([i_p], "ts", T.ki[:, 0:1], T.pI[:], 15, None, A.bitwise_and)
+    V([], "ts", T.ki[:, 1:2], T.pI[:], 4, None, A.logical_shift_right)
+    V([], "ts", T.ki[:, 2:3], T.pI[:], 15, 1, A.bitwise_and, A.logical_shift_right)
+    V([], "ts", T.ki[:, 3:4], T.pI[:], 1, None, A.bitwise_and)
+    c = V([], "copy", T.ki[:, 4:5], T.pI[:])
+    c = V([c], "copy", T.kf[:, 0:5], T.ki[:, 0:5])
+    p15, pd, ph, podd, pp = [T.kf[:, k:k + 1] for k in range(5)]
+    V([c, i_r16], "ts", T.e2[:], T.r16[:, 0:8], ph, None, A.is_equal)
+    V([], "ts", T.eq16[:], T.r16[:], p15, None, A.is_equal)
+    V([], "ts", T.ev[:], podd, 0.0, None, A.is_equal)
+    c_bias = V([], "ts", T.bias[:], p15, -4096.0, 2048.0, A.mult, A.add)
+    c_b4 = V([c_bias, i_mg], "ts", T.b4[:], T.mg[:], pd, 4096.0, A.is_equal, A.mult)
+    for b in range(8):
+        c_sel = V([], "ts", T.sel2[:, b * 128:(b + 1) * 128], T.mg[:], pd, T.e2[:, b:b + 1], A.is_equal, A.mult)
+    c_id = V([i_mm], "ts", T.ident[:], T.mm[:], pp, None, A.is_equal)
+    V([], "ts", T.ki[:, 5:6], T.pI[:], 112, None, A.bitwise_and)
+    c = V([("vq", cnt["v"])], "copy", T.kf[:, 5:6], T.ki[:, 5:6])
+    c = V([c], "ts", T.t1[:], T.mm[:], T.kf[:, 5:6], None, A.subtract)
+    need("v", c)
+    for f in range(16):
+        c_blk = V([], "ts", T.blk[:, f * 128:(f + 1) * 128], T.t1[:], float(f), -16384.0, A.is_equal, A.mult)
+
+    h = V([("ldpar", 16)], "ts", T.hi32[:], T.pr[:], 8, None, A.logical_shift_right)
+    h = V([h], "copy", T.hif[:], T.hi32[:])
+    V([("ldtok", 16)], "ts", T.tok2[:, 0:256], T.tk[:], -2048.0, T.ev[:], A.add, A.mult)
+    V([], "ts", T.tok2[:, 256:512], T.tk[:], -2048.0, podd, A.add, A.mult)
+    hx = []
+    need("v", h)
+    for half in range(2):
+        for f in range(16):
+            o = half * 2048 + f
+            d = V([], "ts", T.hx[:, o:half * 2048 + 2048:16], T.hif[:, half * 128:(half + 1) * 128],
+                  T.eq16[:, f:f + 1], None, A.mult)
+        hx.append(d)
+    l = V([], "ts", T.lo32[:], T.pr[:], 255, None, A.bitwise_and)
+    l = V([l], "copy", T.offl[:], T.lo32[:])
+    c_parc = V([], "ts", T.parc[:], T.pr[:], -2048.0, None, A.add)
+    mx = V([("ld%d" % rank, 16)], "copy", T.pmx[:, 0:256], T.bs[:, rank * 256:(rank + 1) * 256])
+
+    z1 = S([c_zt], T.kvo[:, 0:16], T.zt[:, 0:16], F.Silu)
+    z2 = S([], T.kvp[:, 0:16], T.zt[:, 0:16], F.Silu)
+    for k in range(8):
+        c_ns = S([], T.ns[:, k * 514:(k + 1) * 514], T.zt[:], F.Copy)
+    keyc = []
+    for b in range(8):
+        pk = T["pk%d" % (b % 4)]
+        dep = [c_sel, hx[b // 4]] + ([keyc[b - 4]] if b >= 4 else [])
+        P(dep, pk[:], T.sel2[:, b * 128:(b + 1) * 128], T.tok2[:], True, False)
+        m = P([], pk[:], T.b4[:], T.hx[:, b * 512:(b + 1) * 512], False, True)
+        keyc.append(S([m, c_bias], T.key[:, b * 512:(b + 1) * 512], pk[:], F.Identity, bias=T.bias[:]))
+
+    srcs = near + far[::-1]
+    for k, r in enumerate(srcs):
+        i0 = T.pmx[:, (k % 2) * 256:(k % 2) * 256 + 256]
+        o = T.mxi[:] if k == len(srcs) - 1 else T.pmx[:, 256 - (k % 2) * 256:512 - (k % 2) * 256]
+        mx = V([mx, ("arr%d" % r, n_arr)], "tt", o, i0, T.land[:, r * 256:(r + 1) * 256], A.max)
+    t = V([mx], "ts", T.tgt[:], T.mxi[:], 4095, None, A.bitwise_and)
+
+    zs, mins, scs = [], [], []
+
+    def gather(k):
+        a, b = CHUNKS[k]
+        x = V([t, l, keyc[(16 * b - 1) // 512]], "tt", T.xx[:, 16 * a:16 * b],
+              T.tgt[:, 0:256].indirect(T.offl[:, a:b]), T.key[:, 16 * a:16 * b], A.is_equal)
+        pz = T["pz%d" % (k % 3)][:, 0:b - a]
+        P([c_parc, c_id] + ([mins[k - 3]] if k >= 3 else []), pz, T.ident[:], T.parc[:, a:b], True, False)
+        need("t", x, c_blk)
+        for f in range(16):
+            z = P([], pz, T.blk[:, f * 128:(f + 1) * 128], T.xx[:, 16 * a + f:16 * b:16], False, f == 15)
+        zs.append(z)
+
+    def post(k):
+        a, b = CHUNKS[k]
+        pz = T["pz%d" % (k % 3)][:, 0:b - a]
+        m = V([zs[k], i_dm], "tt", T.uu[:, a:b], pz, T.dumpm[:, a:b], A.min)
+        mins.append(m)
+        o = V([m], "ts", T.off[:, a:b], T.uu[:, a:b], 18448.0, None, A.add)
+        if b <= NSC:
+            dep = [o, c_ns, [i_v0, i_v1, i_v2][k]] + scs[-1:]
+            scs.append(S(dep, T.ns[:, 0:WD].indirect(T.off[:, a:b]), T.vals[:, 16 * a:16 * b], F.Silu))
+        return o
+
+    def vscat(k, dep):
+        a, b = CHUNKS[k]
+        n = 16 * (b - a)
+        return V(dep, "ts", T.nv[:, 0:WD].indirect(T.off[:, a:b]), T.vals[:, 64:64 + n], 1.0, float(16 * a - 64),
+                 A.mult, A.add)
+
+    gather(0)
+    gather(1)
+    post(0)
+    gather(2)
+    post(1)
+    gather(3)
+    post(2)
+    gather(4)
+    o3 = post(3)
+    sc = vscat(3, [o3, i_nv, i_v1, ("zf", 64)])
+    o4 = post(4)
+    mk = V([i_s64], "ts", T.mask[:], T.s64[:], p15, None, A.is_equal)
+    w = V([i_r4], "ts", T.ofw[:, 0:4], T.r4[:], p15, None, A.add)
+    sc = vscat(4, [o4, sc])
+
+    need("y", c_zt, ("sent", n_sent))
+    for k in range(4):
+        g.sync.dma_start(T.nv[:, k * 514:(k + 1) * 514], T.zt[:]).then_inc(T.sem.zf, 16)
+    g.sync.dma_start(T.kvo[:, 16:W], T.kv[:, io * 4096:(io + 1) * 4096]).then_inc(T.sem.kva, 16)
+    g.sync.dma_start(T.kvp[:, 16:W], T.kv[:, ip * 4096:(ip + 1) * 4096]).then_inc(T.sem.kvb, 16)
+
+    def ycols(i, d):
+        return T.yy[:, i * 512 + d:(i + 1) * 512:8]
+
+    S([("kva", 16)], ycols(io, 0), T.kvo[:, 16:80], F.Copy)
+    need("v", mk, sc, scs[-1])
+    rid, pid, _ = topo.addr(T.cores[mate])
+    for d in range(7):
+        ind = T.ofw[:, 4 * d:4 * d + 4]
+        V([w], "tt", T.rm[:, 0:128:2], T.nv[:, 0:W].indirect(ind), T.mask[:], A.mult)
+        r = V([], "tt", T.rm[:, 1:128:2], T.ns[:, 0:W].indirect(ind), T.mask[:], A.mult)
+        for k in range(4):
+            e = V([r], "red", T.rd[:, k:k + 1], T.rm[:, 32 * k:32 * k + 32], AxisListType.X, A.add)
+        w = V([e], "ts", T.ofw[:, 4 * d + 4:4 * d + 8], T.rd[:], 15.25, None, A.add)
+        own = S([w], ycols(io, d + 1), T.kvo[:, 0:W].indirect(T.ofw[:, 4 * d + 4:4 * d + 8]), F.Copy)
+        if d == 4:
+            need("g", w)
+            g.remote_dma(T.la[:], T.ofw[:, 4:24], T.sem.arA, T.sem.lsent, pid, rid, list_mask)
+        if d == 6:
+            need("g", w)
+            g.remote_dma(T.lb[:], T.ofw[:, 24:32], T.sem.arB, T.sem.lsent, pid, rid, list_mask)
+    need("y", own)
+    g.sync.dma_start(T.y[:, io * 512:(io + 1) * 512], T.yy[:, io * 512:(io + 1) * 512]).then_inc(T.sem.st, 16)
+
+    S([("kvb", 16)], ycols(ip, 0), T.kvp[:, 16:80], F.Copy)
+    need("v", ("kvb", 16), z2)
+    for d in (1, 2, 3):
+        V([("arA", n_list)], "copy", ycols(ip, d), T.kvp[:, 0:W].indirect(T.la[:, 4 * d - 4:4 * d]))
+    for d in (4, 5):
+        S([("arA", n_list)], ycols(ip, d), T.kvp[:, 0:W].indirect(T.la[:, 4 * d - 4:4 * d]), F.Copy)
+    a6 = V([("arB", n_list)], "copy", ycols(ip, 6), T.kvp[:, 0:W].indirect(T.lb[:, 0:4]))
+    a7 = S([("arB", n_list)], ycols(ip, 7), T.kvp[:, 0:W].indirect(T.lb[:, 4:8]), F.Copy)
+    need("y", a6, a7)
+    g.sync.dma_start(T.y[:, ip * 512:(ip + 1) * 512], T.yy[:, ip * 512:(ip + 1) * 512]).then_inc(T.sem.st, 16)
+    need("g", ("lsent", 2 * n_list), ("st", 32))
+    for q in ("v", "s", "t", "g"):
+        need("g", (SN[q], cnt[q]))

@@ -1,22 +1,23 @@
 from concourse.bass import DstId, RemoteDMATransfer
-from concourse.mybir import AluOpType as A, AxisListType, ActivationFunctionType as F
+from concourse.mybir import AluOpType as A, ActivationFunctionType as F
 
-NSC = 176
-CHUNKS = [(4, 36), (36, 88), (88, 176), (176, 216), (216, 256)]
+CHUNKS = [(4, 28), (28, 76), (76, 128), (128, 180), (180, 220), (220, 256)]
+SCALAR = (0, 1, 2, 3)
+NZ = 4
+FV = 1
 W = 4112
 WD = 8320
+NSC = CHUNKS[SCALAR[-1]][1]
 SCRATCH = {
     "bs": ("sbuf", [128, 1024], "int32"),
     "land": ("sbuf", [128, 1024], "int32"),
+    "pt": ("sbuf", [128, 512], "int32"),
     "pr": ("sbuf", [128, 256], "int32"),
-    "tk": ("sbuf", [128, 256], "int32"),
-    "hi32": ("sbuf", [128, 256], "int32"),
     "lo32": ("sbuf", [128, 256], "int32"),
-    "hif": ("sbuf", [128, 256], "float16"),
+    "hif": ("sbuf", [128, 512], "float16"),
     "parc": ("sbuf", [128, 256], "float16"),
     "offl": ("sbuf", [128, 256], "uint16"),
-    "tok2": ("sbuf", [128, 512], "float16"),
-    "hx": ("sbuf", [128, 4096], "float16"),
+    "hx": ("sbuf", [128, 2048], "float16"),
     "key": ("sbuf", [128, 4096], "float32"),
     "xx": ("sbuf", [128, 4096], "bfloat16"),
     "mxi": ("sbuf", [128, 256], "int32"),
@@ -24,19 +25,17 @@ SCRATCH = {
     "pI": ("sbuf", [128, 1], "int32"),
     "ki": ("sbuf", [128, 8], "int32"),
     "kf": ("sbuf", [128, 8], "float32"),
-    "ev": ("sbuf", [128, 1], "float32"),
     "bias": ("sbuf", [128, 1], "float32"),
     "r16": ("sbuf", [128, 16], "bfloat16"),
-    "eq16": ("sbuf", [128, 16], "float32"),
-    "e2": ("sbuf", [128, 8], "float32"),
+    "e4": ("sbuf", [128, 4], "float32"),
+    "wc": ("sbuf", [128, 8], "float32"),
     "mg": ("sbuf", [128, 128], "bfloat16"),
-    "mm": ("sbuf", [128, 128], "bfloat16"),
-    "t1": ("sbuf", [128, 128], "bfloat16"),
+    "mm": ("sbuf", [128, 144], "bfloat16"),
     "ident": ("sbuf", [128, 128], "float16"),
-    "b4": ("sbuf", [128, 128], "float16"),
-    "sel2": ("sbuf", [128, 1024], "float16"),
-    "blk": ("sbuf", [128, 2048], "bfloat16"),
+    "sel": ("sbuf", [128, 1024], "float16"),
+    "blk": ("sbuf", [128, 144], "bfloat16"),
     "s64": ("sbuf", [128, 64], "bfloat16"),
+    "s32": ("sbuf", [128, 128], "bfloat16"),
     "mask": ("sbuf", [128, 64], "float32"),
     "r4": ("sbuf", [128, 4], "float32"),
     "dumpm": ("sbuf", [128, 256], "float32"),
@@ -47,7 +46,8 @@ SCRATCH = {
     "ns": ("sbuf", [128, WD], "float32"),
     "nv": ("sbuf", [128, WD], "float32"),
     "rm": ("sbuf", [128, 128], "float32"),
-    "rd": ("sbuf", [128, 4], "float32"),
+    "seg": ("sbuf", [128, 128], "float32"),
+    "rs": ("sbuf", [128, 128], "float32"),
     "ofw": ("sbuf", [128, 32], "uint16"),
     "la": ("sbuf", [128, 20], "uint16"),
     "lb": ("sbuf", [128, 8], "uint16"),
@@ -60,7 +60,7 @@ for _i in range(4):
     SCRATCH["pk%d" % _i] = ("psum", [128, 512], "float32")
 for _i in range(3):
     SCRATCH["pz%d" % _i] = ("psum", [128, 512], "float32")
-SEMAPHORES = (["vq", "sq", "tq", "gq", "sent", "lsent", "arA", "arB", "ldpar", "ldtok", "kva", "kvb", "zf", "st"]
+SEMAPHORES = (["vq", "sq", "tq", "gq", "sent", "lsent", "arA", "arB", "ldpar", "ldlist", "ldtok", "kva", "kvb", "zf", "st"]
               + ["ld%d" % i for i in range(4)] + ["arr%d" % i for i in range(4)])
 
 
@@ -97,7 +97,7 @@ def rank_program(g, core, T, topo):
 
     def V(deps, name, *args, **kw):
         v = g.vector
-        fn = {"copy": v.tensor_copy, "tt": v.tensor_tensor, "ts": v.tensor_scalar, "red": v.tensor_reduce,
+        fn = {"copy": v.tensor_copy, "tt": v.tensor_tensor, "ts": v.tensor_scalar, "scan": v.tensor_tensor_scan,
               "set": v.memset}[name]
         return do("v", deps, fn, *args, **kw)
 
@@ -108,106 +108,134 @@ def rank_program(g, core, T, topo):
         return do("t", deps, g.tensor.matmul, *args)
 
     peers = [r for r in range(N) if r != rank]
-    far = [mate] + [r for r in peers if r != mate and topo.die(T.cores[r]) != topo.die(core)]
-    near = [r for r in peers if r not in far]
-    order = far + near
-    eng = {}
+    others = sorted((r for r in peers if r != mate), key=lambda r: topo.die(T.cores[r]) == topo.die(core))
+    order = [mate] + others
     es = topo.engines(core, T.cores[mate])
-    step = len(es) // 2
-    eng[order[0]] = es[0:step:2]
-    eng[order[1]] = es[step:2 * step:2]
-    eng[order[2]] = es[1:step:2]
-    list_mask = bits(eng[order[0]] + eng[order[1]])
-    n_list = len(eng[order[0]] + eng[order[1]])
+    eng = {order[0]: es, order[1]: es[0::2], order[2]: es[1::2]}
+    n_arr = {order[0]: len(es), order[1]: len(es) // 2, order[2]: len(es) // 2}
+    n_sent = sum(n_arr[r] for r in peers)
+    n_list = len(es)
 
-    for r in order + [rank]:
-        g.sync.dma_start(T.bs[:, r * 256:(r + 1) * 256], T.best[:, r * 4096:(r + 1) * 4096]).then_inc(T.sem["ld%d" % r], 16)
-    g.scalar.dma_start(T.pr[:], T.par[:]).then_inc(T.sem.ldpar, 16)
-    g.scalar.dma_start(T.tk[:], T.tok[:]).then_inc(T.sem.ldtok, 16)
+    def load(queue, dst, src, sem):
+        queue.dma_start(dst, src).then_inc(T.sem[sem], 16)
+
+    def load_best(r):
+        load(g.sync, T.bs[:, r * 256:(r + 1) * 256], T.best[:, r * 4096:(r + 1) * 4096], "ld%d" % r)
+
+    load(g.scalar, T.pt[0:32, :], T.par[:, 0:128], "ldpar")
+    load(g.scalar, T.pt[32:64, :], T.par[:, 128:256], "ldpar")
+    load(g.scalar, T.pt[64:128, :], T.tok[:], "ldtok")
+    for r in order:
+        load_best(r)
+    load(g.sync, T.pr[:], T.par[:], "ldlist")
+    load_best(rank)
 
     fl = {"allow_small_or_imprecise_dtypes": True}
     i_p = do("g", [], g.iota, T.pI[:], [[1, 1]], 0, 1)
     i_r16 = do("g", [], g.iota, T.r16[:], [[1, 16]], 0, 0, **fl)
     i_mg = do("g", [], g.iota, T.mg[:], [[1, 8], [0, 16]], 0, 0, **fl)
-    i_mm = do("g", [], g.iota, T.mm[:], [[1, 128]], 0, 0, **fl)
-    i_v0 = do("g", [], g.iota, T.vals[:, 64:576], [[1, 512]], 65, 0, **fl)
-    need("g", *[("ld%d" % r, 16) for r in order])
-    tr = []
-    for r in order:
-        rid, pid, _ = topo.addr(T.cores[r])
-        tr.append(RemoteDMATransfer(dst_ids=[DstId(rid=rid, pnc=pid)], dma_engine_mask=bits(eng[r]),
-                                    remote_sem=T.sem["arr%d" % rank], src=T.bs[:, r * 256:(r + 1) * 256],
-                                    dst=T.land[:, rank * 256:(rank + 1) * 256]))
-    g.remote_dma_fused(tr, local_sem=T.sem.sent)
-    n_sent = sum(len(eng[r]) for r in order)
-    n_arr = len(eng[order[0]])
+    i_mm = do("g", [], g.iota, T.mm[:], [[1, 144]], -15, 0, **fl)
+
+    def send(rs):
+        need("g", *[("ld%d" % r, 16) for r in rs])
+        tr = []
+        for r in rs:
+            rid, pid, _ = topo.addr(T.cores[r])
+            tr.append(RemoteDMATransfer(dst_ids=[DstId(rid=rid, pnc=pid)], dma_engine_mask=bits(eng[r]),
+                                        remote_sem=T.sem["arr%d" % rank], src=T.bs[:, r * 256:(r + 1) * 256],
+                                        dst=T.land[:, rank * 256:(rank + 1) * 256]))
+        g.remote_dma_fused(tr, local_sem=T.sem.sent)
+
+    send(order[:1])
+    send(order[1:])
+    i_v = {}
+
+    def values(k):
+        a, b = CHUNKS[k]
+        i_v[k] = do("g", [], g.iota, T.vals[:, 16 * a:16 * b], [[1, 16 * (b - a)]], 16 * a + 1, 0, **fl)
+
+    values(SCALAR[0])
     i_dm = do("g", [], g.iota, T.dumpm[:], [[16, 256]], -14336, 1, **fl)
+    for k in SCALAR[1:3]:
+        values(k)
     i_s64 = do("g", [], g.iota, T.s64[:], [[0, 4], [1, 16]], 0, 0, **fl)
     i_r4 = do("g", [], g.iota, T.r4[:], [[16, 4]], 16, 0, **fl)
-    i_v1 = do("g", [], g.iota, T.vals[:, 576:88 * 16], [[1, 88 * 16 - 576]], 577, 0, **fl)
-    i_v2 = do("g", [], g.iota, T.vals[:, 88 * 16:NSC * 16], [[1, (NSC - 88) * 16]], 88 * 16 + 1, 0, **fl)
-    i_nv = do("g", [], g.iota, T.nv[:, 2056:W], [[0, W - 2056]], 0, 0, **fl)
+    i_sg = do("g", [], g.iota, T.s32[:], [[0, 4], [1, 32]], 0, 0, **fl)
+    for k in SCALAR[3:]:
+        values(k)
+    i_nv = do("g", [], g.iota, T.nv[:, 3084:W], [[0, W - 3084]], 0, 0, **fl)
 
     c_zt = V([], "set", T.zt[:], 0.0)
+    V([], "set", T.wc[0:32, 0:4], 4096.0)
+    V([], "set", T.wc[0:32, 4:8], 0.0)
+    V([], "set", T.wc[32:64, 0:4], 0.0)
+    V([], "set", T.wc[32:64, 4:8], 4096.0)
     V([i_p], "ts", T.ki[:, 0:1], T.pI[:], 15, None, A.bitwise_and)
-    V([], "ts", T.ki[:, 1:2], T.pI[:], 4, None, A.logical_shift_right)
-    V([], "ts", T.ki[:, 2:3], T.pI[:], 15, 1, A.bitwise_and, A.logical_shift_right)
-    V([], "ts", T.ki[:, 3:4], T.pI[:], 1, None, A.bitwise_and)
+    V([], "ts", T.ki[0:64, 1:2], T.pI[0:64, :], 31, 2, A.bitwise_and, A.logical_shift_right)
+    V([], "ts", T.ki[64:128, 1:2], T.pI[64:128, :], 63, 3, A.bitwise_and, A.logical_shift_right)
+    V([], "ts", T.ki[0:64, 2:3], T.pI[0:64, :], 3, None, A.bitwise_and)
+    V([], "ts", T.ki[64:128, 2:3], T.pI[64:128, :], 7, None, A.bitwise_and)
+    V([], "ts", T.ki[:, 3:4], T.pI[:], 112, None, A.bitwise_and)
     c = V([], "copy", T.ki[:, 4:5], T.pI[:])
     c = V([c], "copy", T.kf[:, 0:5], T.ki[:, 0:5])
-    p15, pd, ph, podd, pp = [T.kf[:, k:k + 1] for k in range(5)]
-    V([c, i_r16], "ts", T.e2[:], T.r16[:, 0:8], ph, None, A.is_equal)
-    V([], "ts", T.eq16[:], T.r16[:], p15, None, A.is_equal)
-    V([], "ts", T.ev[:], podd, 0.0, None, A.is_equal)
+    p15, pg, p112, pp = [T.kf[:, k:k + 1] for k in (0, 1, 3, 4)]
+    need("v", c, i_r16)
+    c_e4 = V([], "ts", T.e4[0:64, :], T.r16[0:64, 0:4], T.kf[0:64, 2:3], None, A.is_equal)
+    c_wc = V([], "ts", T.wc[64:128, :], T.r16[64:128, 0:8], T.kf[64:128, 2:3], None, A.is_equal)
     c_bias = V([], "ts", T.bias[:], p15, -4096.0, 2048.0, A.mult, A.add)
-    c_b4 = V([c_bias, i_mg], "ts", T.b4[:], T.mg[:], pd, 4096.0, A.is_equal, A.mult)
-    for b in range(8):
-        c_sel = V([], "ts", T.sel2[:, b * 128:(b + 1) * 128], T.mg[:], pd, T.e2[:, b:b + 1], A.is_equal, A.mult)
-    c_id = V([i_mm], "ts", T.ident[:], T.mm[:], pp, None, A.is_equal)
-    V([], "ts", T.ki[:, 5:6], T.pI[:], 112, None, A.bitwise_and)
-    c = V([("vq", cnt["v"])], "copy", T.kf[:, 5:6], T.ki[:, 5:6])
-    c = V([c], "ts", T.t1[:], T.mm[:], T.kf[:, 5:6], None, A.subtract)
-    need("v", c)
-    for f in range(16):
-        c_blk = V([], "ts", T.blk[:, f * 128:(f + 1) * 128], T.t1[:], float(f), -16384.0, A.is_equal, A.mult)
+    fills = []
+    for k in range(FV):
+        fills.append(V([], "set", T.ns[:, k * 514:(k + 1) * 514], 0.0))
+    f_nv = V([], "set", T.nv[:, 2056:2570], 0.0)
 
-    h = V([("ldpar", 16)], "ts", T.hi32[:], T.pr[:], 8, None, A.logical_shift_right)
-    h = V([h], "copy", T.hif[:], T.hi32[:])
-    V([("ldtok", 16)], "ts", T.tok2[:, 0:256], T.tk[:], -2048.0, T.ev[:], A.add, A.mult)
-    V([], "ts", T.tok2[:, 256:512], T.tk[:], -2048.0, podd, A.add, A.mult)
-    hx = []
-    need("v", h)
-    for half in range(2):
-        for f in range(16):
-            o = half * 2048 + f
-            d = V([], "ts", T.hx[:, o:half * 2048 + 2048:16], T.hif[:, half * 128:(half + 1) * 128],
-                  T.eq16[:, f:f + 1], None, A.mult)
-        hx.append(d)
-    l = V([], "ts", T.lo32[:], T.pr[:], 255, None, A.bitwise_and)
-    l = V([l], "copy", T.offl[:], T.lo32[:])
+    h = V([("ldpar", 32)], "ts", T.hif[0:64, :], T.pt[0:64, :], 1.0 / 256, 1025.0 - 127.5 / 256, A.mult, A.add)
+    need("v", h, c_e4)
+    for f in range(16):
+        c_hx = V([], "ts", T.hx[0:64, f:2048:16], T.hif[0:64, (f % 4) * 128:(f % 4 + 1) * 128],
+                 -1025.0, T.e4[0:64, f // 4:f // 4 + 1], A.add, A.mult)
+    need("v", c_wc)
+    c_sel = []
+
+    def select(b):
+        c_sel.append(V([i_mg], "ts", T.sel[:, b * 128:(b + 1) * 128], T.mg[:], pg, T.wc[:, b:b + 1], A.is_equal, A.mult))
+
+    select(0)
+    select(1)
+    t0 = V([("ldtok", 16)], "ts", T.hx[64:128, 0:512], T.pt[64:128, :], -2048.0, None, A.add)
+    c_tok = [t0]
+    for b in range(1, 4):
+        c_tok.append(V([t0], "copy", T.hx[64:128, b * 512:(b + 1) * 512], T.hx[64:128, 0:512]))
+        if b < 3:
+            select(b + 1)
+    for b in range(4, 8):
+        select(b)
+    l = V([("ldlist", 16)], "ts", T.lo32[:], T.pr[:], 255, None, A.bitwise_and)
     c_parc = V([], "ts", T.parc[:], T.pr[:], -2048.0, None, A.add)
+    l = V([l], "copy", T.offl[:], T.lo32[:])
+    c_id = V([i_mm], "ts", T.ident[:], T.mm[:, 15:143], pp, None, A.is_equal)
+    c_blk = V([], "ts", T.blk[:], T.mm[:], p112, -16384.0, A.is_equal, A.mult)
     mx = V([("ld%d" % rank, 16)], "copy", T.pmx[:, 0:256], T.bs[:, rank * 256:(rank + 1) * 256])
 
     z1 = S([c_zt], T.kvo[:, 0:16], T.zt[:, 0:16], F.Silu)
     z2 = S([], T.kvp[:, 0:16], T.zt[:, 0:16], F.Silu)
-    for k in range(8):
-        c_ns = S([], T.ns[:, k * 514:(k + 1) * 514], T.zt[:], F.Copy)
+    for k in range(FV, 8):
+        fills.append(S([], T.ns[:, k * 514:(k + 1) * 514], T.zt[:], F.Copy))
     keyc = []
     for b in range(8):
         pk = T["pk%d" % (b % 4)]
-        dep = [c_sel, hx[b // 4]] + ([keyc[b - 4]] if b >= 4 else [])
-        P(dep, pk[:], T.sel2[:, b * 128:(b + 1) * 128], T.tok2[:], True, False)
-        m = P([], pk[:], T.b4[:], T.hx[:, b * 512:(b + 1) * 512], False, True)
+        m = P([c_sel[b], c_hx, c_tok[b % 4]] + ([keyc[b - 4]] if b >= 4 else []), pk[:],
+              T.sel[:, b * 128:(b + 1) * 128], T.hx[:, (b % 4) * 512:(b % 4 + 1) * 512], True, True)
         keyc.append(S([m, c_bias], T.key[:, b * 512:(b + 1) * 512], pk[:], F.Identity, bias=T.bias[:]))
+    s_nv = S([], T.nv[:, 2570:3084], T.zt[:], F.Copy)
 
-    srcs = near + far[::-1]
+    srcs = [mate] + others[::-1]
     for k, r in enumerate(srcs):
         i0 = T.pmx[:, (k % 2) * 256:(k % 2) * 256 + 256]
         o = T.mxi[:] if k == len(srcs) - 1 else T.pmx[:, 256 - (k % 2) * 256:512 - (k % 2) * 256]
-        mx = V([mx, ("arr%d" % r, n_arr)], "tt", o, i0, T.land[:, r * 256:(r + 1) * 256], A.max)
+        mx = V([mx, ("arr%d" % r, n_arr[r])], "tt", o, i0, T.land[:, r * 256:(r + 1) * 256], A.max)
     t = V([mx], "ts", T.tgt[:], T.mxi[:], 4095, None, A.bitwise_and)
 
-    zs, mins, scs = [], [], []
+    zs, mins, scs, vsc = [], [], [], []
 
     def gather(k):
         a, b = CHUNKS[k]
@@ -217,7 +245,7 @@ def rank_program(g, core, T, topo):
         P([c_parc, c_id] + ([mins[k - 3]] if k >= 3 else []), pz, T.ident[:], T.parc[:, a:b], True, False)
         need("t", x, c_blk)
         for f in range(16):
-            z = P([], pz, T.blk[:, f * 128:(f + 1) * 128], T.xx[:, 16 * a + f:16 * b:16], False, f == 15)
+            z = P([], pz, T.blk[:, 15 - f:143 - f], T.xx[:, 16 * a + f:16 * b:16], False, f == 15)
         zs.append(z)
 
     def post(k):
@@ -226,58 +254,56 @@ def rank_program(g, core, T, topo):
         m = V([zs[k], i_dm], "tt", T.uu[:, a:b], pz, T.dumpm[:, a:b], A.min)
         mins.append(m)
         o = V([m], "ts", T.off[:, a:b], T.uu[:, a:b], 18448.0, None, A.add)
-        if b <= NSC:
-            dep = [o, c_ns, [i_v0, i_v1, i_v2][k]] + scs[-1:]
-            scs.append(S(dep, T.ns[:, 0:WD].indirect(T.off[:, a:b]), T.vals[:, 16 * a:16 * b], F.Silu))
+        if k in SCALAR:
+            scs.append(S([o, i_v[k]] + fills + scs[-1:], T.ns[:, 0:WD].indirect(T.off[:, a:b]),
+                         T.vals[:, 16 * a:16 * b], F.Silu))
         return o
 
     def vscat(k, dep):
         a, b = CHUNKS[k]
         n = 16 * (b - a)
-        return V(dep, "ts", T.nv[:, 0:WD].indirect(T.off[:, a:b]), T.vals[:, 64:64 + n], 1.0, float(16 * a - 64),
-                 A.mult, A.add)
+        vsc.append(V([dep, i_nv, f_nv, s_nv, ("zf", 16 * NZ)] + [i_v[c] for c in SCALAR if 16 * CHUNKS[c][0] < 64 + n]
+                     + vsc[-1:], "ts", T.nv[:, 0:WD].indirect(T.off[:, a:b]), T.vals[:, 64:64 + n],
+                     1.0, float(16 * a - 64), A.mult, A.add))
 
+    last = len(CHUNKS) - 1
     gather(0)
-    gather(1)
-    post(0)
-    gather(2)
-    post(1)
-    gather(3)
-    post(2)
-    gather(4)
-    o3 = post(3)
-    sc = vscat(3, [o3, i_nv, i_v1, ("zf", 64)])
-    o4 = post(4)
+    for k in range(1, last + 1):
+        gather(k)
+        o = post(k - 1)
+        if k - 1 not in SCALAR:
+            vscat(k - 1, o)
+    o = post(last)
+    V([i_sg], "ts", T.seg[:], T.s32[:], 0.5, None, A.is_gt)
     mk = V([i_s64], "ts", T.mask[:], T.s64[:], p15, None, A.is_equal)
     w = V([i_r4], "ts", T.ofw[:, 0:4], T.r4[:], p15, None, A.add)
-    sc = vscat(4, [o4, sc])
+    vscat(last, o)
 
     need("y", c_zt, ("sent", n_sent))
-    for k in range(4):
+    for k in range(NZ):
         g.sync.dma_start(T.nv[:, k * 514:(k + 1) * 514], T.zt[:]).then_inc(T.sem.zf, 16)
-    g.sync.dma_start(T.kvo[:, 16:W], T.kv[:, io * 4096:(io + 1) * 4096]).then_inc(T.sem.kva, 16)
-    g.sync.dma_start(T.kvp[:, 16:W], T.kv[:, ip * 4096:(ip + 1) * 4096]).then_inc(T.sem.kvb, 16)
+    load(g.sync, T.kvo[:, 16:W], T.kv[:, io * 4096:(io + 1) * 4096], "kva")
+    load(g.sync, T.kvp[:, 16:W], T.kv[:, ip * 4096:(ip + 1) * 4096], "kvb")
 
     def ycols(i, d):
         return T.yy[:, i * 512 + d:(i + 1) * 512:8]
 
-    S([("kva", 16)], ycols(io, 0), T.kvo[:, 16:80], F.Copy)
-    need("v", mk, sc, scs[-1])
+    S([("kva", 16), z1], ycols(io, 0), T.kvo[:, 16:80], F.Copy)
+    need("v", mk, vsc[-1], scs[-1])
     rid, pid, _ = topo.addr(T.cores[mate])
     for d in range(7):
         ind = T.ofw[:, 4 * d:4 * d + 4]
         V([w], "tt", T.rm[:, 0:128:2], T.nv[:, 0:W].indirect(ind), T.mask[:], A.mult)
         r = V([], "tt", T.rm[:, 1:128:2], T.ns[:, 0:W].indirect(ind), T.mask[:], A.mult)
-        for k in range(4):
-            e = V([r], "red", T.rd[:, k:k + 1], T.rm[:, 32 * k:32 * k + 32], AxisListType.X, A.add)
-        w = V([e], "ts", T.ofw[:, 4 * d + 4:4 * d + 8], T.rd[:], 15.25, None, A.add)
+        e = V([r], "scan", T.rs[:], T.seg[:], T.rm[:], 0.0, A.mult, A.add)
+        w = V([e], "ts", T.ofw[:, 4 * d + 4:4 * d + 8], T.rs[:, 31:128:32], 15.25, None, A.add)
         own = S([w], ycols(io, d + 1), T.kvo[:, 0:W].indirect(T.ofw[:, 4 * d + 4:4 * d + 8]), F.Copy)
         if d == 4:
             need("g", w)
-            g.remote_dma(T.la[:], T.ofw[:, 4:24], T.sem.arA, T.sem.lsent, pid, rid, list_mask)
+            g.remote_dma(T.la[:], T.ofw[:, 4:24], T.sem.arA, T.sem.lsent, pid, rid, bits(es))
         if d == 6:
             need("g", w)
-            g.remote_dma(T.lb[:], T.ofw[:, 24:32], T.sem.arB, T.sem.lsent, pid, rid, list_mask)
+            g.remote_dma(T.lb[:], T.ofw[:, 24:32], T.sem.arB, T.sem.lsent, pid, rid, bits(es))
     need("y", own)
     g.sync.dma_start(T.y[:, io * 512:(io + 1) * 512], T.yy[:, io * 512:(io + 1) * 512]).then_inc(T.sem.st, 16)
 

@@ -3,8 +3,8 @@ from concourse.mybir import AluOpType as A, ActivationFunctionType as F
 
 CHUNKS = [(4, 28), (28, 76), (76, 128), (128, 180), (180, 220), (220, 256)]
 SCALAR = (0, 1, 2, 3)
+ORDER = "g0 g1 m0 c0 o0 g2 m1 c1 o1 g3 m2 g4 o2 m3 g5 o3 m4 c2 o4 s4 m5 o5 s5"
 NZ = 4
-FV = 1
 W = 4112
 WD = 8320
 NSC = CHUNKS[SCALAR[-1]][1]
@@ -34,10 +34,10 @@ SCRATCH = {
     "ident": ("sbuf", [128, 128], "float16"),
     "sel": ("sbuf", [128, 1024], "float16"),
     "blk": ("sbuf", [128, 144], "bfloat16"),
-    "s64": ("sbuf", [128, 64], "bfloat16"),
     "s32": ("sbuf", [128, 128], "bfloat16"),
-    "mask": ("sbuf", [128, 64], "float32"),
-    "r4": ("sbuf", [128, 4], "float32"),
+    "w2": ("sbuf", [128, 1], "float32"),
+    "corr": ("sbuf", [128, 1], "float32"),
+    "sk": ("sbuf", [128, 128], "float32"),
     "dumpm": ("sbuf", [128, 256], "float32"),
     "vals": ("sbuf", [128, NSC * 16], "float32"),
     "zt": ("sbuf", [128, 514], "float32"),
@@ -60,8 +60,8 @@ for _i in range(4):
     SCRATCH["pk%d" % _i] = ("psum", [128, 512], "float32")
 for _i in range(3):
     SCRATCH["pz%d" % _i] = ("psum", [128, 512], "float32")
-SEMAPHORES = (["vq", "sq", "tq", "gq", "sent", "lsent", "arA", "arB", "ldpar", "ldlist", "ldtok", "kva", "kvb", "zf", "st"]
-              + ["ld%d" % i for i in range(4)] + ["arr%d" % i for i in range(4)])
+SEMAPHORES = (["vq", "sq", "tq", "gq", "sent", "lsent", "arA", "arB", "ldpar", "ldlist", "ldtok", "kva", "kvb", "zf", "zn",
+               "st"] + ["ld%d" % i for i in range(4)] + ["arr%d" % i for i in range(4)])
 
 
 def bits(engines):
@@ -112,8 +112,8 @@ def rank_program(g, core, T, topo):
     order = [mate] + others
     es = topo.engines(core, T.cores[mate])
     eng = {order[0]: es, order[1]: es[0::2], order[2]: es[1::2]}
-    n_arr = {order[0]: len(es), order[1]: len(es) // 2, order[2]: len(es) // 2}
-    n_sent = sum(n_arr[r] for r in peers)
+    n_arr = {r: len(eng[r]) for r in order}
+    n_sent = sum(n_arr[r] for r in order)
     n_list = len(es)
 
     def load(queue, dst, src, sem):
@@ -135,6 +135,7 @@ def rank_program(g, core, T, topo):
     i_r16 = do("g", [], g.iota, T.r16[:], [[1, 16]], 0, 0, **fl)
     i_mg = do("g", [], g.iota, T.mg[:], [[1, 8], [0, 16]], 0, 0, **fl)
     i_mm = do("g", [], g.iota, T.mm[:], [[1, 144]], -15, 0, **fl)
+    i_sg = do("g", [], g.iota, T.s32[:], [[0, 4], [1, 32]], 0, 0, **fl)
 
     def send(rs):
         need("g", *[("ld%d" % r, 16) for r in rs])
@@ -156,14 +157,9 @@ def rank_program(g, core, T, topo):
 
     values(SCALAR[0])
     i_dm = do("g", [], g.iota, T.dumpm[:], [[16, 256]], -14336, 1, **fl)
-    for k in SCALAR[1:3]:
+    for k in SCALAR[1:]:
         values(k)
-    i_s64 = do("g", [], g.iota, T.s64[:], [[0, 4], [1, 16]], 0, 0, **fl)
-    i_r4 = do("g", [], g.iota, T.r4[:], [[16, 4]], 16, 0, **fl)
-    i_sg = do("g", [], g.iota, T.s32[:], [[0, 4], [1, 32]], 0, 0, **fl)
-    for k in SCALAR[3:]:
-        values(k)
-    i_nv = do("g", [], g.iota, T.nv[:, 3084:W], [[0, W - 3084]], 0, 0, **fl)
+    i_nv = do("g", [], g.iota, T.nv[:, 2570:W], [[0, W - 2570]], 0, 0, **fl)
 
     c_zt = V([], "set", T.zt[:], 0.0)
     V([], "set", T.wc[0:32, 0:4], 4096.0)
@@ -183,9 +179,13 @@ def rank_program(g, core, T, topo):
     c_e4 = V([], "ts", T.e4[0:64, :], T.r16[0:64, 0:4], T.kf[0:64, 2:3], None, A.is_equal)
     c_wc = V([], "ts", T.wc[64:128, :], T.r16[64:128, 0:8], T.kf[64:128, 2:3], None, A.is_equal)
     c_bias = V([], "ts", T.bias[:], p15, -4096.0, 2048.0, A.mult, A.add)
-    fills = []
-    for k in range(FV):
-        fills.append(V([], "set", T.ns[:, k * 514:(k + 1) * 514], 0.0))
+    V([], "ts", T.w2[:], p15, 524288.0, 262144.0, A.mult, A.add)
+    c_id = V([i_mm], "ts", T.ident[:], T.mm[:, 15:143], pp, None, A.is_equal)
+    c_blk = V([], "ts", T.blk[:], T.mm[:], p112, -16384.0, A.is_equal, A.mult)
+    c_sel = []
+    need("v", c_wc)
+    for b in range(8):
+        c_sel.append(V([i_mg], "ts", T.sel[:, b * 128:(b + 1) * 128], T.mg[:], pg, T.wc[:, b:b + 1], A.is_equal, A.mult))
     f_nv = V([], "set", T.nv[:, 2056:2570], 0.0)
 
     h = V([("ldpar", 32)], "ts", T.hif[0:64, :], T.pt[0:64, :], 1.0 / 256, 1025.0 - 127.5 / 256, A.mult, A.add)
@@ -193,49 +193,39 @@ def rank_program(g, core, T, topo):
     for f in range(16):
         c_hx = V([], "ts", T.hx[0:64, f:2048:16], T.hif[0:64, (f % 4) * 128:(f % 4 + 1) * 128],
                  -1025.0, T.e4[0:64, f // 4:f // 4 + 1], A.add, A.mult)
-    need("v", c_wc)
-    c_sel = []
-
-    def select(b):
-        c_sel.append(V([i_mg], "ts", T.sel[:, b * 128:(b + 1) * 128], T.mg[:], pg, T.wc[:, b:b + 1], A.is_equal, A.mult))
-
-    select(0)
-    select(1)
     t0 = V([("ldtok", 16)], "ts", T.hx[64:128, 0:512], T.pt[64:128, :], -2048.0, None, A.add)
     c_tok = [t0]
     for b in range(1, 4):
         c_tok.append(V([t0], "copy", T.hx[64:128, b * 512:(b + 1) * 512], T.hx[64:128, 0:512]))
-        if b < 3:
-            select(b + 1)
-    for b in range(4, 8):
-        select(b)
     l = V([("ldlist", 16)], "ts", T.lo32[:], T.pr[:], 255, None, A.bitwise_and)
     c_parc = V([], "ts", T.parc[:], T.pr[:], -2048.0, None, A.add)
     l = V([l], "copy", T.offl[:], T.lo32[:])
-    c_id = V([i_mm], "ts", T.ident[:], T.mm[:, 15:143], pp, None, A.is_equal)
-    c_blk = V([], "ts", T.blk[:], T.mm[:], p112, -16384.0, A.is_equal, A.mult)
     mx = V([("ld%d" % rank, 16)], "copy", T.pmx[:, 0:256], T.bs[:, rank * 256:(rank + 1) * 256])
 
     z1 = S([c_zt], T.kvo[:, 0:16], T.zt[:, 0:16], F.Silu)
     z2 = S([], T.kvp[:, 0:16], T.zt[:, 0:16], F.Silu)
-    for k in range(FV, 8):
-        fills.append(S([], T.ns[:, k * 514:(k + 1) * 514], T.zt[:], F.Copy))
+    fills = [("zn", 16)]
+    for k in range(512, W, 450):
+        fills.append(S([], T.ns[:, k:k + 450], T.zt[:, 0:450], F.Copy))
     keyc = []
     for b in range(8):
         pk = T["pk%d" % (b % 4)]
         m = P([c_sel[b], c_hx, c_tok[b % 4]] + ([keyc[b - 4]] if b >= 4 else []), pk[:],
               T.sel[:, b * 128:(b + 1) * 128], T.hx[:, (b % 4) * 512:(b % 4 + 1) * 512], True, True)
         keyc.append(S([m, c_bias], T.key[:, b * 512:(b + 1) * 512], pk[:], F.Identity, bias=T.bias[:]))
-    s_nv = S([], T.nv[:, 2570:3084], T.zt[:], F.Copy)
 
-    srcs = [mate] + others[::-1]
-    for k, r in enumerate(srcs):
-        i0 = T.pmx[:, (k % 2) * 256:(k % 2) * 256 + 256]
-        o = T.mxi[:] if k == len(srcs) - 1 else T.pmx[:, 256 - (k % 2) * 256:512 - (k % 2) * 256]
-        mx = V([mx, ("arr%d" % r, n_arr[r])], "tt", o, i0, T.land[:, r * 256:(r + 1) * 256], A.max)
-    t = V([mx], "ts", T.tgt[:], T.mxi[:], 4095, None, A.bitwise_and)
+    first, second, third = [mate] + others[::-1]
+    mx = V([mx, ("arr%d" % first, n_arr[first])], "tt", T.pmx[:, 256:512], T.pmx[:, 0:256],
+           T.land[:, first * 256:(first + 1) * 256], A.max)
+    hm = {0: mx, 128: mx}
+    for r, o, i in ((second, T.pmx, 256), (third, T.mxi, 0)):
+        for c in hm:
+            hm[c] = V([hm[c], ("arr%d" % r, n_arr[r])], "tt", o[:, c:c + 128], T.pmx[:, i + c:i + c + 128],
+                      T.land[:, r * 256 + c:r * 256 + c + 128], A.max)
+    for c in hm:
+        t = V([hm[c]], "ts", T.tgt[:, c:c + 128], T.mxi[:, c:c + 128], 4095, None, A.bitwise_and)
 
-    zs, mins, scs, vsc = [], [], [], []
+    zs, mins, scs, vsc, offs, con = [], [], [], [], [], []
 
     def gather(k):
         a, b = CHUNKS[k]
@@ -248,75 +238,90 @@ def rank_program(g, core, T, topo):
             z = P([], pz, T.blk[:, 15 - f:143 - f], T.xx[:, 16 * a + f:16 * b:16], False, f == 15)
         zs.append(z)
 
-    def post(k):
+    def lowest(k):
         a, b = CHUNKS[k]
         pz = T["pz%d" % (k % 3)][:, 0:b - a]
-        m = V([zs[k], i_dm], "tt", T.uu[:, a:b], pz, T.dumpm[:, a:b], A.min)
-        mins.append(m)
-        o = V([m], "ts", T.off[:, a:b], T.uu[:, a:b], 18448.0, None, A.add)
+        mins.append(V([zs[k], i_dm], "tt", T.uu[:, a:b], pz, T.dumpm[:, a:b], A.min))
+
+    def offsets(k):
+        a, b = CHUNKS[k]
+        o = V([mins[k]], "ts", T.off[:, a:b], T.uu[:, a:b], 18448.0, None, A.add)
+        offs.append(o)
         if k in SCALAR:
             scs.append(S([o, i_v[k]] + fills + scs[-1:], T.ns[:, 0:WD].indirect(T.off[:, a:b]),
                          T.vals[:, 16 * a:16 * b], F.Silu))
-        return o
 
-    def vscat(k, dep):
+    def vscat(k):
         a, b = CHUNKS[k]
         n = 16 * (b - a)
-        vsc.append(V([dep, i_nv, f_nv, s_nv, ("zf", 16 * NZ)] + [i_v[c] for c in SCALAR if 16 * CHUNKS[c][0] < 64 + n]
+        vsc.append(V([offs[k], i_nv, f_nv, ("zf", 16 * NZ)] + [i_v[c] for c in SCALAR if 16 * CHUNKS[c][0] < 64 + n]
                      + vsc[-1:], "ts", T.nv[:, 0:WD].indirect(T.off[:, a:b]), T.vals[:, 64:64 + n],
                      1.0, float(16 * a - 64), A.mult, A.add))
 
-    last = len(CHUNKS) - 1
-    gather(0)
-    for k in range(1, last + 1):
-        gather(k)
-        o = post(k - 1)
-        if k - 1 not in SCALAR:
-            vscat(k - 1, o)
-    o = post(last)
-    V([i_sg], "ts", T.seg[:], T.s32[:], 0.5, None, A.is_gt)
-    mk = V([i_s64], "ts", T.mask[:], T.s64[:], p15, None, A.is_equal)
-    w = V([i_r4], "ts", T.ofw[:, 0:4], T.r4[:], p15, None, A.add)
-    vscat(last, o)
+    def consts(k):
+        if k == 0:
+            con.append(V([i_sg], "ts", T.sk[:], T.s32[:], 262144.0, None, A.mult))
+        elif k == 1:
+            con.append(V(con[-1:], "ts", T.seg[:], T.sk[:], T.w2[:], 8192.0, A.subtract, A.min))
+        else:
+            con.append(V([], "ts", T.corr[:], p15, 16384.0, 15.25 - 245760.0, A.mult, A.add))
 
-    need("y", c_zt, ("sent", n_sent))
+    step = {"g": gather, "m": lowest, "o": offsets, "s": vscat, "c": consts}
+    for word in ORDER.split():
+        step[word[0]](int(word[1:]))
+
+    need("y", c_zt, ("arr%d" % mate, n_arr[mate]))
+    load(g.sync, T.ns[:, 0:512], T.zt[:, 0:512], "zn")
     for k in range(NZ):
-        g.sync.dma_start(T.nv[:, k * 514:(k + 1) * 514], T.zt[:]).then_inc(T.sem.zf, 16)
+        load(g.sync, T.nv[:, k * 514:(k + 1) * 514], T.zt[:], "zf")
     load(g.sync, T.kvo[:, 16:W], T.kv[:, io * 4096:(io + 1) * 4096], "kva")
     load(g.sync, T.kvp[:, 16:W], T.kv[:, ip * 4096:(ip + 1) * 4096], "kvb")
 
     def ycols(i, d):
         return T.yy[:, i * 512 + d:(i + 1) * 512:8]
 
-    S([("kva", 16), z1], ycols(io, 0), T.kvo[:, 16:80], F.Copy)
-    need("v", mk, vsc[-1], scs[-1])
+    def own_keys(*levels):
+        for d in levels:
+            if d:
+                o = S([("kva", 16), z1], ycols(io, d), T.kvo[:, 0:W].indirect(T.ofw[:, 4 * d:4 * d + 4]), F.Copy)
+            else:
+                o = S([("kva", 16)], ycols(io, 0), T.kvo[:, 16:80], F.Copy)
+        return o
+
+    need("v", con[-1], vsc[-1])
+    need("s", scs[-1])
     rid, pid, _ = topo.addr(T.cores[mate])
     for d in range(7):
-        ind = T.ofw[:, 4 * d:4 * d + 4]
-        V([w], "tt", T.rm[:, 0:128:2], T.nv[:, 0:W].indirect(ind), T.mask[:], A.mult)
-        r = V([], "tt", T.rm[:, 1:128:2], T.ns[:, 0:W].indirect(ind), T.mask[:], A.mult)
-        e = V([r], "scan", T.rs[:], T.seg[:], T.rm[:], 0.0, A.mult, A.add)
-        w = V([e], "ts", T.ofw[:, 4 * d + 4:4 * d + 8], T.rs[:, 31:128:32], 15.25, None, A.add)
-        own = S([w], ycols(io, d + 1), T.kvo[:, 0:W].indirect(T.ofw[:, 4 * d + 4:4 * d + 8]), F.Copy)
+        if d:
+            ind = T.ofw[:, 4 * d:4 * d + 4]
+            r1 = V([w], "copy", T.rm[:, 0:128:2], T.nv[:, 0:W].indirect(ind))
+            r2 = S([w], T.rm[:, 1:128:2], T.ns[:, 0:W].indirect(ind), F.Copy)
+        else:
+            r1 = V([], "copy", T.rm[:, 0:128:2], T.nv[:, 16:80])
+            r2 = S([], T.rm[:, 1:128:2], T.ns[:, 16:80], F.Copy)
+        e = V([r1, r2], "scan", T.rs[:], T.seg[:], T.rm[:], 0.0, A.add, A.max)
+        w = V([e], "ts", T.ofw[:, 4 * d + 4:4 * d + 8], T.rs[:, 31:128:32], T.corr[:], None, A.add)
         if d == 4:
             need("g", w)
             g.remote_dma(T.la[:], T.ofw[:, 4:24], T.sem.arA, T.sem.lsent, pid, rid, bits(es))
         if d == 6:
             need("g", w)
             g.remote_dma(T.lb[:], T.ofw[:, 24:32], T.sem.arB, T.sem.lsent, pid, rid, bits(es))
-    need("y", own)
-    g.sync.dma_start(T.y[:, io * 512:(io + 1) * 512], T.yy[:, io * 512:(io + 1) * 512]).then_inc(T.sem.st, 16)
+        if d >= 4:
+            own_keys(2 * d - 8, 2 * d - 7)
+    need("s", w)
+    need("y", own_keys(6, 7))
+    load(g.sync, T.y[:, io * 512:(io + 1) * 512], T.yy[:, io * 512:(io + 1) * 512], "st")
 
     S([("kvb", 16)], ycols(ip, 0), T.kvp[:, 16:80], F.Copy)
     need("v", ("kvb", 16), z2)
-    for d in (1, 2, 3):
+    for d in (1, 2, 3, 4):
         V([("arA", n_list)], "copy", ycols(ip, d), T.kvp[:, 0:W].indirect(T.la[:, 4 * d - 4:4 * d]))
-    for d in (4, 5):
-        S([("arA", n_list)], ycols(ip, d), T.kvp[:, 0:W].indirect(T.la[:, 4 * d - 4:4 * d]), F.Copy)
+    S([("arA", n_list)], ycols(ip, 5), T.kvp[:, 0:W].indirect(T.la[:, 16:20]), F.Copy)
     a6 = V([("arB", n_list)], "copy", ycols(ip, 6), T.kvp[:, 0:W].indirect(T.lb[:, 0:4]))
     a7 = S([("arB", n_list)], ycols(ip, 7), T.kvp[:, 0:W].indirect(T.lb[:, 4:8]), F.Copy)
     need("y", a6, a7)
-    g.sync.dma_start(T.y[:, ip * 512:(ip + 1) * 512], T.yy[:, ip * 512:(ip + 1) * 512]).then_inc(T.sem.st, 16)
-    need("g", ("lsent", 2 * n_list), ("st", 32))
+    load(g.sync, T.y[:, ip * 512:(ip + 1) * 512], T.yy[:, ip * 512:(ip + 1) * 512], "st")
+    need("g", ("sent", n_sent), ("lsent", 2 * n_list), ("st", 32))
     for q in ("v", "s", "t", "g"):
         need("g", (SN[q], cnt[q]))

@@ -1,10 +1,13 @@
 from concourse.bass import DstId, RemoteDMATransfer
 from concourse.mybir import AluOpType as A, ActivationFunctionType as F
 
-CHUNKS = [(4, 28), (28, 76), (76, 128), (128, 180), (180, 220), (220, 256)]
+CHUNKS = [(4, 26), (26, 76), (76, 124), (124, 176), (176, 220), (220, 256)]
 SCALAR = (0, 1, 2, 3)
-ORDER = "g0 g1 m0 c0 o0 g2 m1 c1 o1 g3 m2 g4 o2 m3 g5 o3 m4 c2 o4 s4 m5 o5 s5"
+ORDER = "c0 g0 g1 m0 c1 o0 g2 m1 c2 o1 g3 m2 g4 o2 m3 g5 o3 m4 o4 s4 m5 o5 s5"
+OWN = [[], [], [], [0], [1], [2], [3]]
+OWN_V, OWN_S = [4, 5], [6, 7]
 NZ = 4
+ZG = 2568
 W = 4112
 WD = 8320
 NSC = CHUNKS[SCALAR[-1]][1]
@@ -34,10 +37,10 @@ SCRATCH = {
     "ident": ("sbuf", [128, 128], "float16"),
     "sel": ("sbuf", [128, 1024], "float16"),
     "blk": ("sbuf", [128, 144], "bfloat16"),
-    "s32": ("sbuf", [128, 128], "bfloat16"),
+    "s32": ("sbuf", [128, 64], "bfloat16"),
     "w2": ("sbuf", [128, 1], "float32"),
     "corr": ("sbuf", [128, 1], "float32"),
-    "sk": ("sbuf", [128, 128], "float32"),
+    "sk": ("sbuf", [128, 64], "float32"),
     "dumpm": ("sbuf", [128, 256], "float32"),
     "vals": ("sbuf", [128, NSC * 16], "float32"),
     "zt": ("sbuf", [128, 514], "float32"),
@@ -46,7 +49,7 @@ SCRATCH = {
     "ns": ("sbuf", [128, WD], "float32"),
     "nv": ("sbuf", [128, WD], "float32"),
     "rm": ("sbuf", [128, 128], "float32"),
-    "seg": ("sbuf", [128, 128], "float32"),
+    "seg": ("sbuf", [128, 64], "float32"),
     "rs": ("sbuf", [128, 128], "float32"),
     "ofw": ("sbuf", [128, 32], "uint16"),
     "la": ("sbuf", [128, 20], "uint16"),
@@ -135,7 +138,7 @@ def rank_program(g, core, T, topo):
     i_r16 = do("g", [], g.iota, T.r16[:], [[1, 16]], 0, 0, **fl)
     i_mg = do("g", [], g.iota, T.mg[:], [[1, 8], [0, 16]], 0, 0, **fl)
     i_mm = do("g", [], g.iota, T.mm[:], [[1, 144]], -15, 0, **fl)
-    i_sg = do("g", [], g.iota, T.s32[:], [[0, 4], [1, 32]], 0, 0, **fl)
+    i_sg = do("g", [], g.iota, T.s32[:], [[0, 2], [1, 32]], 0, 0, **fl)
 
     def send(rs):
         need("g", *[("ld%d" % r, 16) for r in rs])
@@ -159,7 +162,7 @@ def rank_program(g, core, T, topo):
     i_dm = do("g", [], g.iota, T.dumpm[:], [[16, 256]], -14336, 1, **fl)
     for k in SCALAR[1:]:
         values(k)
-    i_nv = do("g", [], g.iota, T.nv[:, 2570:W], [[0, W - 2570]], 0, 0, **fl)
+    i_nv = do("g", [], g.iota, T.nv[:, ZG:W], [[0, W - ZG]], 0, 0, **fl)
 
     c_zt = V([], "set", T.zt[:], 0.0)
     V([], "set", T.wc[0:32, 0:4], 4096.0)
@@ -186,7 +189,6 @@ def rank_program(g, core, T, topo):
     need("v", c_wc)
     for b in range(8):
         c_sel.append(V([i_mg], "ts", T.sel[:, b * 128:(b + 1) * 128], T.mg[:], pg, T.wc[:, b:b + 1], A.is_equal, A.mult))
-    f_nv = V([], "set", T.nv[:, 2056:2570], 0.0)
 
     h = V([("ldpar", 32)], "ts", T.hif[0:64, :], T.pt[0:64, :], 1.0 / 256, 1025.0 - 127.5 / 256, A.mult, A.add)
     need("v", h, c_e4)
@@ -194,16 +196,15 @@ def rank_program(g, core, T, topo):
         c_hx = V([], "ts", T.hx[0:64, f:2048:16], T.hif[0:64, (f % 4) * 128:(f % 4 + 1) * 128],
                  -1025.0, T.e4[0:64, f // 4:f // 4 + 1], A.add, A.mult)
     t0 = V([("ldtok", 16)], "ts", T.hx[64:128, 0:512], T.pt[64:128, :], -2048.0, None, A.add)
+    l = V([("ldlist", 16)], "ts", T.lo32[:], T.pr[:], 255, None, A.bitwise_and)
     c_tok = [t0]
     for b in range(1, 4):
         c_tok.append(V([t0], "copy", T.hx[64:128, b * 512:(b + 1) * 512], T.hx[64:128, 0:512]))
-    l = V([("ldlist", 16)], "ts", T.lo32[:], T.pr[:], 255, None, A.bitwise_and)
-    c_parc = V([], "ts", T.parc[:], T.pr[:], -2048.0, None, A.add)
-    l = V([l], "copy", T.offl[:], T.lo32[:])
     mx = V([("ld%d" % rank, 16)], "copy", T.pmx[:, 0:256], T.bs[:, rank * 256:(rank + 1) * 256])
+    l = V([l], "copy", T.offl[:], T.lo32[:])
+    c_parc = V([], "ts", T.parc[:], T.pr[:], -2048.0, None, A.add)
 
-    z1 = S([c_zt], T.kvo[:, 0:16], T.zt[:, 0:16], F.Silu)
-    z2 = S([], T.kvp[:, 0:16], T.zt[:, 0:16], F.Silu)
+    z1 = S([c_zt], T.kvo[:, 0:8], T.zt[:, 0:8], F.Silu)
     fills = [("zn", 16)]
     for k in range(512, W, 450):
         fills.append(S([], T.ns[:, k:k + 450], T.zt[:, 0:450], F.Copy))
@@ -213,19 +214,19 @@ def rank_program(g, core, T, topo):
         m = P([c_sel[b], c_hx, c_tok[b % 4]] + ([keyc[b - 4]] if b >= 4 else []), pk[:],
               T.sel[:, b * 128:(b + 1) * 128], T.hx[:, (b % 4) * 512:(b % 4 + 1) * 512], True, True)
         keyc.append(S([m, c_bias], T.key[:, b * 512:(b + 1) * 512], pk[:], F.Identity, bias=T.bias[:]))
+    f_nv = S([], T.nv[:, NZ * 514:ZG], T.zt[:, 0:ZG - NZ * 514], F.Copy)
 
     first, second, third = [mate] + others[::-1]
-    mx = V([mx, ("arr%d" % first, n_arr[first])], "tt", T.pmx[:, 256:512], T.pmx[:, 0:256],
-           T.land[:, first * 256:(first + 1) * 256], A.max)
     hm = {0: mx, 128: mx}
-    for r, o, i in ((second, T.pmx, 256), (third, T.mxi, 0)):
+    for r, o, to, at in ((first, T.pmx, 256, 0), (second, T.pmx, 0, 256), (third, T.mxi, 0, 0)):
         for c in hm:
-            hm[c] = V([hm[c], ("arr%d" % r, n_arr[r])], "tt", o[:, c:c + 128], T.pmx[:, i + c:i + c + 128],
+            hm[c] = V([hm[c], ("arr%d" % r, n_arr[r])], "tt", o[:, to + c:to + c + 128], T.pmx[:, at + c:at + c + 128],
                       T.land[:, r * 256 + c:r * 256 + c + 128], A.max)
     for c in hm:
         t = V([hm[c]], "ts", T.tgt[:, c:c + 128], T.mxi[:, c:c + 128], 4095, None, A.bitwise_and)
 
     zs, mins, scs, vsc, offs, con = [], [], [], [], [], []
+    zkeys = []
 
     def gather(k):
         a, b = CHUNKS[k]
@@ -250,6 +251,9 @@ def rank_program(g, core, T, topo):
         if k in SCALAR:
             scs.append(S([o, i_v[k]] + fills + scs[-1:], T.ns[:, 0:WD].indirect(T.off[:, a:b]),
                          T.vals[:, 16 * a:16 * b], F.Silu))
+            if len(scs) < 4:
+                d = (T.kvo[:, 8:16], T.kvp[:, 0:8], T.kvp[:, 8:16])[len(scs) - 1]
+                zkeys.append(S([], d, T.zt[:, 0:8], F.Copy))
 
     def vscat(k):
         a, b = CHUNKS[k]
@@ -277,44 +281,56 @@ def rank_program(g, core, T, topo):
     load(g.sync, T.kvo[:, 16:W], T.kv[:, io * 4096:(io + 1) * 4096], "kva")
     load(g.sync, T.kvp[:, 16:W], T.kv[:, ip * 4096:(ip + 1) * 4096], "kvb")
 
+    lists = {}
+
     def ycols(i, d):
         return T.yy[:, i * 512 + d:(i + 1) * 512:8]
 
-    def own_keys(*levels):
-        for d in levels:
-            if d:
-                o = S([("kva", 16), z1], ycols(io, d), T.kvo[:, 0:W].indirect(T.ofw[:, 4 * d:4 * d + 4]), F.Copy)
-            else:
-                o = S([("kva", 16)], ycols(io, 0), T.kvo[:, 16:80], F.Copy)
-        return o
+    def own_key(q, d):
+        dep = [("kva", 16), z1] + zkeys[:1]
+        if d:
+            dep.append(lists[d])
+        src = T.kvo[:, 0:W].indirect(T.ofw[:, 4 * d:4 * d + 4]) if d else T.kvo[:, 16:80]
+        return V(dep, "copy", ycols(io, d), src) if q == "v" else S(dep, ycols(io, d), src, F.Copy)
 
     need("v", con[-1], vsc[-1])
     need("s", scs[-1])
     rid, pid, _ = topo.addr(T.cores[mate])
+    w = [None, None]
     for d in range(7):
-        if d:
-            ind = T.ofw[:, 4 * d:4 * d + 4]
-            r1 = V([w], "copy", T.rm[:, 0:128:2], T.nv[:, 0:W].indirect(ind))
-            r2 = S([w], T.rm[:, 1:128:2], T.ns[:, 0:W].indirect(ind), F.Copy)
-        else:
-            r1 = V([], "copy", T.rm[:, 0:128:2], T.nv[:, 16:80])
-            r2 = S([], T.rm[:, 1:128:2], T.ns[:, 16:80], F.Copy)
-        e = V([r1, r2], "scan", T.rs[:], T.seg[:], T.rm[:], 0.0, A.add, A.max)
-        w = V([e], "ts", T.ofw[:, 4 * d + 4:4 * d + 8], T.rs[:, 31:128:32], T.corr[:], None, A.add)
+        r1, r2, e = [None, None], [None, None], [None, None]
+        for h in (0, 1):
+            c = 4 * d + 2 * h
+            ev, od = T.rm[:, 64 * h:64 * h + 64:2], T.rm[:, 64 * h + 1:64 * h + 64:2]
+            if d:
+                r1[h] = V([w[h]], "copy", ev, T.nv[:, 0:W].indirect(T.ofw[:, c:c + 2]))
+                r2[h] = S([w[h]], od, T.ns[:, 0:W].indirect(T.ofw[:, c:c + 2]), F.Copy)
+            else:
+                r1[h] = V([], "copy", ev, T.nv[:, 16 + 32 * h:48 + 32 * h])
+                r2[h] = S([], od, T.ns[:, 16 + 32 * h:48 + 32 * h], F.Copy)
+        for h in (0, 1):
+            e[h] = V([r1[h], r2[h]], "scan", T.rs[:, 64 * h:64 * h + 64], T.seg[:], T.rm[:, 64 * h:64 * h + 64], 0.0,
+                     A.add, A.max)
+        for h in (0, 1):
+            c = 4 * d + 4 + 2 * h
+            w[h] = V([e[h]], "ts", T.ofw[:, c:c + 2], T.rs[:, 64 * h + 31:64 * h + 64:32], T.corr[:], None, A.add)
+        lists[d + 1] = w[1]
         if d == 4:
-            need("g", w)
+            need("g", w[1])
             g.remote_dma(T.la[:], T.ofw[:, 4:24], T.sem.arA, T.sem.lsent, pid, rid, bits(es))
         if d == 6:
-            need("g", w)
+            need("g", w[1])
             g.remote_dma(T.lb[:], T.ofw[:, 24:32], T.sem.arB, T.sem.lsent, pid, rid, bits(es))
-        if d >= 4:
-            own_keys(2 * d - 8, 2 * d - 7)
-    need("s", w)
-    need("y", own_keys(6, 7))
+        for k in OWN[d]:
+            own_key("s", k)
+    a1 = [own_key("v", k) for k in OWN_V]
+    a2 = [own_key("s", k) for k in OWN_S]
+    need("y", a1[-1], a2[-1])
     load(g.sync, T.y[:, io * 512:(io + 1) * 512], T.yy[:, io * 512:(io + 1) * 512], "st")
 
+    need("s", zkeys[-1])
     S([("kvb", 16)], ycols(ip, 0), T.kvp[:, 16:80], F.Copy)
-    need("v", ("kvb", 16), z2)
+    need("v", ("kvb", 16), zkeys[-1])
     for d in (1, 2, 3, 4):
         V([("arA", n_list)], "copy", ycols(ip, d), T.kvp[:, 0:W].indirect(T.la[:, 4 * d - 4:4 * d]))
     S([("arA", n_list)], ycols(ip, 5), T.kvp[:, 0:W].indirect(T.la[:, 16:20]), F.Copy)

from concourse.bass import DstId, RemoteDMATransfer
from concourse.mybir import AluOpType as A, ActivationFunctionType as F

CHUNKS = [(4, 26), (26, 76), (76, 124), (124, 176), (176, 220), (220, 256)]
SCALAR = (0, 1, 2, 3)
ORDER = "c0 g0 g1 m0 c1 o0 g2 m1 c2 o1 g3 m2 g4 o2 m3 g5 o3 m4 o4 s4 m5 o5 s5"
OWN = [[], [], [], [0], [1], [2], [3]]
OWN_V, OWN_S = [4, 5], [6, 7]
NZ = 4
ZG = 2568
W = 4112
WD = 8320
NSC = CHUNKS[SCALAR[-1]][1]
SCRATCH = {
    "bs": ("sbuf", [128, 1024], "int32"),
    "land": ("sbuf", [128, 1024], "int32"),
    "pt": ("sbuf", [128, 512], "int32"),
    "pr": ("sbuf", [128, 256], "int32"),
    "lo32": ("sbuf", [128, 256], "int32"),
    "hif": ("sbuf", [128, 512], "float16"),
    "parc": ("sbuf", [128, 256], "float16"),
    "offl": ("sbuf", [128, 256], "uint16"),
    "hx": ("sbuf", [128, 2048], "float16"),
    "key": ("sbuf", [128, 4096], "float32"),
    "xx": ("sbuf", [128, 4096], "bfloat16"),
    "mxi": ("sbuf", [128, 256], "int32"),
    "tgt": ("sbuf", [128, 256], "int32"),
    "pI": ("sbuf", [128, 1], "int32"),
    "ki": ("sbuf", [128, 8], "int32"),
    "kf": ("sbuf", [128, 8], "float32"),
    "bias": ("sbuf", [128, 1], "float32"),
    "r16": ("sbuf", [128, 16], "bfloat16"),
    "e4": ("sbuf", [128, 4], "float32"),
    "wc": ("sbuf", [128, 8], "float32"),
    "mg": ("sbuf", [128, 128], "bfloat16"),
    "mm": ("sbuf", [128, 144], "bfloat16"),
    "ident": ("sbuf", [128, 128], "float16"),
    "sel": ("sbuf", [128, 1024], "float16"),
    "blk": ("sbuf", [128, 144], "bfloat16"),
    "s32": ("sbuf", [128, 64], "bfloat16"),
    "w2": ("sbuf", [128, 1], "float32"),
    "corr": ("sbuf", [128, 1], "float32"),
    "sk": ("sbuf", [128, 64], "float32"),
    "dumpm": ("sbuf", [128, 256], "float32"),
    "vals": ("sbuf", [128, NSC * 16], "float32"),
    "zt": ("sbuf", [128, 514], "float32"),
    "uu": ("sbuf", [128, 256], "float32"),
    "off": ("sbuf", [128, 256], "uint16"),
    "ns": ("sbuf", [128, WD], "float32"),
    "nv": ("sbuf", [128, WD], "float32"),
    "rm": ("sbuf", [128, 128], "float32"),
    "seg": ("sbuf", [128, 64], "float32"),
    "rs": ("sbuf", [128, 128], "float32"),
    "ofw": ("sbuf", [128, 32], "uint16"),
    "la": ("sbuf", [128, 20], "uint16"),
    "lb": ("sbuf", [128, 8], "uint16"),
    "kvo": ("sbuf", [128, W], "bfloat16"),
    "kvp": ("sbuf", [128, W], "bfloat16"),
    "yy": ("sbuf", [128, 1024], "bfloat16"),
    "pmx": ("psum", [128, 512], "float32"),
}
for _i in range(4):
    SCRATCH["pk%d" % _i] = ("psum", [128, 512], "float32")
for _i in range(3):
    SCRATCH["pz%d" % _i] = ("psum", [128, 512], "float32")
SEMAPHORES = (["vq", "sq", "tq", "gq", "sent", "lsent", "arA", "arB", "ldpar", "ldlist", "ldtok", "kva", "kvb", "zf", "zn",
               "st"] + ["ld%d" % i for i in range(4)] + ["arr%d" % i for i in range(4)])


def bits(engines):
    m = 0
    for e in engines:
        m |= 1 << e
    return m


def rank_program(g, core, T, topo):
    rank = T.rank_of(core)
    if rank is None:
        return
    N = len(T.cores)
    mate = (rank + 2) % N
    io, ip = rank // 2, mate // 2
    Q = {"v": g.vector, "s": g.scalar, "t": g.tensor, "g": g, "y": g.sync}
    SN = {"v": "vq", "s": "sq", "t": "tq", "g": "gq"}
    cnt = {"v": 0, "s": 0, "t": 0, "g": 0}
    seen = {q: {} for q in Q}

    def need(q, *deps):
        for sem, val in deps:
            if seen[q].get(sem, 0) < val:
                Q[q].wait_ge(T.sem[sem], val)
                seen[q][sem] = val

    def do(q, deps, fn, *args, **kw):
        need(q, *deps)
        fn(*args, **kw).then_inc(T.sem[SN[q]], 1)
        cnt[q] += 1
        return (SN[q], cnt[q])

    def V(deps, name, *args, **kw):
        v = g.vector
        fn = {"copy": v.tensor_copy, "tt": v.tensor_tensor, "ts": v.tensor_scalar, "scan": v.tensor_tensor_scan,
              "set": v.memset}[name]
        return do("v", deps, fn, *args, **kw)

    def S(deps, *args, **kw):
        return do("s", deps, g.scalar.activation, *args, **kw)

    def P(deps, *args):
        return do("t", deps, g.tensor.matmul, *args)

    peers = [r for r in range(N) if r != rank]
    others = sorted((r for r in peers if r != mate), key=lambda r: topo.die(T.cores[r]) == topo.die(core))
    order = [mate] + others
    es = topo.engines(core, T.cores[mate])
    eng = {order[0]: es, order[1]: es[0::2], order[2]: es[1::2]}
    n_arr = {r: len(eng[r]) for r in order}
    n_sent = sum(n_arr[r] for r in order)
    n_list = len(es)

    def load(queue, dst, src, sem):
        queue.dma_start(dst, src).then_inc(T.sem[sem], 16)

    def load_best(r):
        load(g.sync, T.bs[:, r * 256:(r + 1) * 256], T.best[:, r * 4096:(r + 1) * 4096], "ld%d" % r)

    load(g.scalar, T.pt[0:32, :], T.par[:, 0:128], "ldpar")
    load(g.scalar, T.pt[32:64, :], T.par[:, 128:256], "ldpar")
    load(g.scalar, T.pt[64:128, :], T.tok[:], "ldtok")
    for r in order:
        load_best(r)
    load(g.sync, T.pr[:], T.par[:], "ldlist")
    load_best(rank)

    fl = {"allow_small_or_imprecise_dtypes": True}
    i_p = do("g", [], g.iota, T.pI[:], [[1, 1]], 0, 1)
    i_r16 = do("g", [], g.iota, T.r16[:], [[1, 16]], 0, 0, **fl)
    i_mg = do("g", [], g.iota, T.mg[:], [[1, 8], [0, 16]], 0, 0, **fl)
    i_mm = do("g", [], g.iota, T.mm[:], [[1, 144]], -15, 0, **fl)
    i_sg = do("g", [], g.iota, T.s32[:], [[0, 2], [1, 32]], 0, 0, **fl)

    def send(rs):
        need("g", *[("ld%d" % r, 16) for r in rs])
        tr = []
        for r in rs:
            rid, pid, _ = topo.addr(T.cores[r])
            tr.append(RemoteDMATransfer(dst_ids=[DstId(rid=rid, pnc=pid)], dma_engine_mask=bits(eng[r]),
                                        remote_sem=T.sem["arr%d" % rank], src=T.bs[:, r * 256:(r + 1) * 256],
                                        dst=T.land[:, rank * 256:(rank + 1) * 256]))
        g.remote_dma_fused(tr, local_sem=T.sem.sent)

    send(order[:1])
    send(order[1:])
    i_v = {}

    def values(k):
        a, b = CHUNKS[k]
        i_v[k] = do("g", [], g.iota, T.vals[:, 16 * a:16 * b], [[1, 16 * (b - a)]], 16 * a + 1, 0, **fl)

    values(SCALAR[0])
    i_dm = do("g", [], g.iota, T.dumpm[:], [[16, 256]], -14336, 1, **fl)
    for k in SCALAR[1:]:
        values(k)
    i_nv = do("g", [], g.iota, T.nv[:, ZG:W], [[0, W - ZG]], 0, 0, **fl)

    c_zt = V([], "set", T.zt[:], 0.0)
    V([], "set", T.wc[0:32, 0:4], 4096.0)
    V([], "set", T.wc[0:32, 4:8], 0.0)
    V([], "set", T.wc[32:64, 0:4], 0.0)
    V([], "set", T.wc[32:64, 4:8], 4096.0)
    V([i_p], "ts", T.ki[:, 0:1], T.pI[:], 15, None, A.bitwise_and)
    V([], "ts", T.ki[0:64, 1:2], T.pI[0:64, :], 31, 2, A.bitwise_and, A.logical_shift_right)
    V([], "ts", T.ki[64:128, 1:2], T.pI[64:128, :], 63, 3, A.bitwise_and, A.logical_shift_right)
    V([], "ts", T.ki[0:64, 2:3], T.pI[0:64, :], 3, None, A.bitwise_and)
    V([], "ts", T.ki[64:128, 2:3], T.pI[64:128, :], 7, None, A.bitwise_and)
    V([], "ts", T.ki[:, 3:4], T.pI[:], 112, None, A.bitwise_and)
    c = V([], "copy", T.ki[:, 4:5], T.pI[:])
    c = V([c], "copy", T.kf[:, 0:5], T.ki[:, 0:5])
    p15, pg, p112, pp = [T.kf[:, k:k + 1] for k in (0, 1, 3, 4)]
    need("v", c, i_r16)
    c_e4 = V([], "ts", T.e4[0:64, :], T.r16[0:64, 0:4], T.kf[0:64, 2:3], None, A.is_equal)
    c_wc = V([], "ts", T.wc[64:128, :], T.r16[64:128, 0:8], T.kf[64:128, 2:3], None, A.is_equal)
    c_bias = V([], "ts", T.bias[:], p15, -4096.0, 2048.0, A.mult, A.add)
    V([], "ts", T.w2[:], p15, 524288.0, 262144.0, A.mult, A.add)
    c_id = V([i_mm], "ts", T.ident[:], T.mm[:, 15:143], pp, None, A.is_equal)
    c_blk = V([], "ts", T.blk[:], T.mm[:], p112, -16384.0, A.is_equal, A.mult)
    c_sel = []
    need("v", c_wc)
    for b in range(8):
        c_sel.append(V([i_mg], "ts", T.sel[:, b * 128:(b + 1) * 128], T.mg[:], pg, T.wc[:, b:b + 1], A.is_equal, A.mult))

    h = V([("ldpar", 32)], "ts", T.hif[0:64, :], T.pt[0:64, :], 1.0 / 256, 1025.0 - 127.5 / 256, A.mult, A.add)
    need("v", h, c_e4)
    for f in range(16):
        c_hx = V([], "ts", T.hx[0:64, f:2048:16], T.hif[0:64, (f % 4) * 128:(f % 4 + 1) * 128],
                 -1025.0, T.e4[0:64, f // 4:f // 4 + 1], A.add, A.mult)
    t0 = V([("ldtok", 16)], "ts", T.hx[64:128, 0:512], T.pt[64:128, :], -2048.0, None, A.add)
    l = V([("ldlist", 16)], "ts", T.lo32[:], T.pr[:], 255, None, A.bitwise_and)
    c_tok = [t0]
    for b in range(1, 4):
        c_tok.append(V([t0], "copy", T.hx[64:128, b * 512:(b + 1) * 512], T.hx[64:128, 0:512]))
    mx = V([("ld%d" % rank, 16)], "copy", T.pmx[:, 0:256], T.bs[:, rank * 256:(rank + 1) * 256])
    l = V([l], "copy", T.offl[:], T.lo32[:])
    c_parc = V([], "ts", T.parc[:], T.pr[:], -2048.0, None, A.add)

    z1 = S([c_zt], T.kvo[:, 0:8], T.zt[:, 0:8], F.Silu)
    fills = [("zn", 16)]
    for k in range(512, W, 450):
        fills.append(S([], T.ns[:, k:k + 450], T.zt[:, 0:450], F.Copy))
    keyc = []
    for b in range(8):
        pk = T["pk%d" % (b % 4)]
        m = P([c_sel[b], c_hx, c_tok[b % 4]] + ([keyc[b - 4]] if b >= 4 else []), pk[:],
              T.sel[:, b * 128:(b + 1) * 128], T.hx[:, (b % 4) * 512:(b % 4 + 1) * 512], True, True)
        keyc.append(S([m, c_bias], T.key[:, b * 512:(b + 1) * 512], pk[:], F.Identity, bias=T.bias[:]))
    f_nv = S([], T.nv[:, NZ * 514:ZG], T.zt[:, 0:ZG - NZ * 514], F.Copy)

    first, second, third = [mate] + others[::-1]
    hm = {0: mx, 128: mx}
    for r, o, to, at in ((first, T.pmx, 256, 0), (second, T.pmx, 0, 256), (third, T.mxi, 0, 0)):
        for c in hm:
            hm[c] = V([hm[c], ("arr%d" % r, n_arr[r])], "tt", o[:, to + c:to + c + 128], T.pmx[:, at + c:at + c + 128],
                      T.land[:, r * 256 + c:r * 256 + c + 128], A.max)
    for c in hm:
        t = V([hm[c]], "ts", T.tgt[:, c:c + 128], T.mxi[:, c:c + 128], 4095, None, A.bitwise_and)

    zs, mins, scs, vsc, offs, con = [], [], [], [], [], []
    zkeys = []

    def gather(k):
        a, b = CHUNKS[k]
        x = V([t, l, keyc[(16 * b - 1) // 512]], "tt", T.xx[:, 16 * a:16 * b],
              T.tgt[:, 0:256].indirect(T.offl[:, a:b]), T.key[:, 16 * a:16 * b], A.is_equal)
        pz = T["pz%d" % (k % 3)][:, 0:b - a]
        P([c_parc, c_id] + ([mins[k - 3]] if k >= 3 else []), pz, T.ident[:], T.parc[:, a:b], True, False)
        need("t", x, c_blk)
        for f in range(16):
            z = P([], pz, T.blk[:, 15 - f:143 - f], T.xx[:, 16 * a + f:16 * b:16], False, f == 15)
        zs.append(z)

    def lowest(k):
        a, b = CHUNKS[k]
        pz = T["pz%d" % (k % 3)][:, 0:b - a]
        mins.append(V([zs[k], i_dm], "tt", T.uu[:, a:b], pz, T.dumpm[:, a:b], A.min))

    def offsets(k):
        a, b = CHUNKS[k]
        o = V([mins[k]], "ts", T.off[:, a:b], T.uu[:, a:b], 18448.0, None, A.add)
        offs.append(o)
        if k in SCALAR:
            scs.append(S([o, i_v[k]] + fills + scs[-1:], T.ns[:, 0:WD].indirect(T.off[:, a:b]),
                         T.vals[:, 16 * a:16 * b], F.Silu))
            if len(scs) < 4:
                d = (T.kvo[:, 8:16], T.kvp[:, 0:8], T.kvp[:, 8:16])[len(scs) - 1]
                zkeys.append(S([], d, T.zt[:, 0:8], F.Copy))

    def vscat(k):
        a, b = CHUNKS[k]
        n = 16 * (b - a)
        vsc.append(V([offs[k], i_nv, f_nv, ("zf", 16 * NZ)] + [i_v[c] for c in SCALAR if 16 * CHUNKS[c][0] < 64 + n]
                     + vsc[-1:], "ts", T.nv[:, 0:WD].indirect(T.off[:, a:b]), T.vals[:, 64:64 + n],
                     1.0, float(16 * a - 64), A.mult, A.add))

    def consts(k):
        if k == 0:
            con.append(V([i_sg], "ts", T.sk[:], T.s32[:], 262144.0, None, A.mult))
        elif k == 1:
            con.append(V(con[-1:], "ts", T.seg[:], T.sk[:], T.w2[:], 8192.0, A.subtract, A.min))
        else:
            con.append(V([], "ts", T.corr[:], p15, 16384.0, 15.25 - 245760.0, A.mult, A.add))

    step = {"g": gather, "m": lowest, "o": offsets, "s": vscat, "c": consts}
    for word in ORDER.split():
        step[word[0]](int(word[1:]))

    need("y", c_zt, ("arr%d" % mate, n_arr[mate]))
    load(g.sync, T.ns[:, 0:512], T.zt[:, 0:512], "zn")
    for k in range(NZ):
        load(g.sync, T.nv[:, k * 514:(k + 1) * 514], T.zt[:], "zf")
    load(g.sync, T.kvo[:, 16:W], T.kv[:, io * 4096:(io + 1) * 4096], "kva")
    load(g.sync, T.kvp[:, 16:W], T.kv[:, ip * 4096:(ip + 1) * 4096], "kvb")

    lists = {}

    def ycols(i, d):
        return T.yy[:, i * 512 + d:(i + 1) * 512:8]

    def own_key(q, d):
        dep = [("kva", 16), z1] + zkeys[:1]
        if d:
            dep.append(lists[d])
        src = T.kvo[:, 0:W].indirect(T.ofw[:, 4 * d:4 * d + 4]) if d else T.kvo[:, 16:80]
        return V(dep, "copy", ycols(io, d), src) if q == "v" else S(dep, ycols(io, d), src, F.Copy)

    need("v", con[-1], vsc[-1])
    need("s", scs[-1])
    rid, pid, _ = topo.addr(T.cores[mate])
    w = [None, None]
    for d in range(7):
        r1, r2, e = [None, None], [None, None], [None, None]
        for h in (0, 1):
            c = 4 * d + 2 * h
            ev, od = T.rm[:, 64 * h:64 * h + 64:2], T.rm[:, 64 * h + 1:64 * h + 64:2]
            if d:
                r1[h] = V([w[h]], "copy", ev, T.nv[:, 0:W].indirect(T.ofw[:, c:c + 2]))
                r2[h] = S([w[h]], od, T.ns[:, 0:W].indirect(T.ofw[:, c:c + 2]), F.Copy)
            else:
                r1[h] = V([], "copy", ev, T.nv[:, 16 + 32 * h:48 + 32 * h])
                r2[h] = S([], od, T.ns[:, 16 + 32 * h:48 + 32 * h], F.Copy)
        for h in (0, 1):
            e[h] = V([r1[h], r2[h]], "scan", T.rs[:, 64 * h:64 * h + 64], T.seg[:], T.rm[:, 64 * h:64 * h + 64], 0.0,
                     A.add, A.max)
        for h in (0, 1):
            c = 4 * d + 4 + 2 * h
            w[h] = V([e[h]], "ts", T.ofw[:, c:c + 2], T.rs[:, 64 * h + 31:64 * h + 64:32], T.corr[:], None, A.add)
        lists[d + 1] = w[1]
        if d == 4:
            need("g", w[1])
            g.remote_dma(T.la[:], T.ofw[:, 4:24], T.sem.arA, T.sem.lsent, pid, rid, bits(es))
        if d == 6:
            need("g", w[1])
            g.remote_dma(T.lb[:], T.ofw[:, 24:32], T.sem.arB, T.sem.lsent, pid, rid, bits(es))
        for k in OWN[d]:
            own_key("s", k)
    a1 = [own_key("v", k) for k in OWN_V]
    a2 = [own_key("s", k) for k in OWN_S]
    need("y", a1[-1], a2[-1])
    load(g.sync, T.y[:, io * 512:(io + 1) * 512], T.yy[:, io * 512:(io + 1) * 512], "st")

    need("s", zkeys[-1])
    S([("kvb", 16)], ycols(ip, 0), T.kvp[:, 16:80], F.Copy)
    need("v", ("kvb", 16), zkeys[-1])
    for d in (1, 2, 3, 4):
        V([("arA", n_list)], "copy", ycols(ip, d), T.kvp[:, 0:W].indirect(T.la[:, 4 * d - 4:4 * d]))
    S([("arA", n_list)], ycols(ip, 5), T.kvp[:, 0:W].indirect(T.la[:, 16:20]), F.Copy)
    a6 = V([("arB", n_list)], "copy", ycols(ip, 6), T.kvp[:, 0:W].indirect(T.lb[:, 0:4]))
    a7 = S([("arB", n_list)], ycols(ip, 7), T.kvp[:, 0:W].indirect(T.lb[:, 4:8]), F.Copy)
    need("y", a6, a7)
    load(g.sync, T.y[:, ip * 512:(ip + 1) * 512], T.yy[:, ip * 512:(ip + 1) * 512], "st")
    need("g", ("sent", n_sent), ("lsent", 2 * n_list), ("st", 32))
    for q in ("v", "s", "t", "g"):
        need("g", (SN[q], cnt[q]))
